import numpy as np
import ml_dtypes


def mxq(x, axis, fmt="e4m3"):
    dtype, down = {"e4m3": (ml_dtypes.float8_e4m3fn, 7), "e5m2": (ml_dtypes.float8_e5m2, 14)}[fmt]
    v = np.moveaxis(np.asarray(x, np.float32).astype(ml_dtypes.bfloat16).astype(np.float64), axis, -1)
    blocks = v.reshape(v.shape[:-1] + (-1, 32))
    amax = np.abs(blocks).max(-1, keepdims=True)
    byte = np.maximum(np.where(amax > 0, np.frexp(amax)[1] - 1 + 127, 0) - down, 1)
    scale = np.exp2(byte - 127.0)
    codes = (blocks / scale).astype(np.float32).astype(dtype).astype(np.float64)
    return np.moveaxis((codes * scale).reshape(v.shape), -1, axis)


WIDE = False


def mx_kscale(k):
    if not WIDE:
        return np.ones(k)
    levels = np.array([10, -10, 5, -5, 0])
    if k % 512:
        return np.exp2(np.random.permutation(np.resize(levels, k // 32))).repeat(32)
    a = np.empty((k // 512, 16))
    for p in range(k // 512):
        a[p, :8] = np.random.permutation(np.resize(levels, 8))
        for g in range(8):
            far = levels[np.abs(levels - a[p, g]) >= 10]
            a[p, g + 8] = far[np.random.randint(len(far))]
    return np.exp2(a.ravel()).repeat(32)


def f64(x):
    return np.asarray(x).astype(np.float64)


def striped(idx):
    return np.tile(np.asarray(idx).reshape(-1, 16).T, (8, 1)).astype(np.uint16)


def unstriped(offs):
    return offs[:16].T.reshape(-1).astype(np.int64)


E2M1 = np.array([0.0, 0.5, 1.0, 1.5, 2.0, 3.0, 4.0, 6.0, -0.0, -0.5, -1.0, -1.5, -2.0, -3.0, -4.0, -6.0])


def pack_weight(w, fmt):
    k, n = w.shape
    w = f64(np.asarray(w, np.float32).astype(ml_dtypes.bfloat16)).reshape(k // 32, 32, n)
    amax = np.abs(w).max(1)
    if fmt == "e4m3":
        byte = np.frexp(amax)[1] - 1 + 127 - 7
    else:
        mant, ex = np.frexp(amax / 6.0)
        byte = np.where(mant > 0.5, ex, ex - 1) + 127
    byte = np.clip(np.where(amax > 0, byte, 1), 1, 254)
    scaled = (w * np.exp2(127.0 - byte)[:, None, :]).reshape(k, n).astype(np.float32)
    by_word = np.ascontiguousarray(scaled.reshape(k // 512, 128, 4, n).transpose(0, 1, 3, 2))
    if fmt == "e4m3":
        words = by_word.astype(ml_dtypes.float8_e4m3fn).view(np.uint8)
    else:
        c = by_word.astype(ml_dtypes.float4_e2m1fn).view(np.uint8) & 0xF
        words = (c[..., 0::2] | (c[..., 1::2] << 4)).reshape(k // 512, 128, 2 * n)
    return np.ascontiguousarray(words), np.ascontiguousarray(byte.astype(np.uint8).reshape(k // 512, 16, n))


def unpack_weight(words, scales, fmt):
    g, _, n = scales.shape
    words = np.ascontiguousarray(words).reshape(g, 128, n, -1)
    if fmt == "e4m3":
        vals = words.view(ml_dtypes.float8_e4m3fn).astype(np.float64)
    else:
        nib = np.empty((g, 128, n, 4), np.uint8)
        nib[..., 0::2] = words & 0xF
        nib[..., 1::2] = words >> 4
        vals = E2M1[nib]
    vals = vals * np.repeat(np.exp2(scales.astype(np.float64) - 127.0), 8, axis=1)[..., None]
    return vals.transpose(0, 1, 3, 2).reshape(g * 512, n)


B, N, T, D, DV, NQ = 1, 512, 1024, 1024, 256, 256
CAP = 2.0


def setup_inputs():
    n = np.random.standard_normal
    idx = np.random.permutation(T)[:B * N]
    s = mx_kscale(D)[:, None]
    u = np.ones(T)
    u[idx] = mx_kscale(B * N)
    r = np.random.uniform(0.5, 2.0, T)
    k = n((D, T)) / s
    v = n((DV, T)) / (u * r)
    kp = pack_weight(k, "e2m1")
    return {
        "qT": (n((B, D, NQ)) * s * (1.00 / np.sqrt(D))).astype(np.float32),
        "k_words": np.ascontiguousarray(kp[0].reshape(D // 1024, 2, 128, T, 2).transpose(0, 2, 3, 1, 4)).reshape(D // 1024, 128, T, 4),
        "k_scales": kp[1],
        "vT": v.astype(np.float32),
        "vs": np.tile(u * r, (128, 1)).astype(np.float32),
        "offs": striped(idx),
    }


def reference(qT, k_words, k_scales, vT, vs, offs):
    idx = unstriped(offs)
    k = unpack_weight(k_words.reshape(D // 1024, 128, T, 2, 2).transpose(0, 3, 1, 2, 4).reshape(D // 512, 128, 2 * T), k_scales, "e2m1")
    v = f64(vT)
    pick = lambda x: x[:, idx].reshape(x.shape[0], B, N).transpose(1, 0, 2)
    q = f64(qT)
    score = mxq(q, 1, "e4m3").transpose(0, 2, 1) @ pick(k)
    score = CAP * np.tanh(score / CAP)
    p = np.square(np.maximum(score, 0.0))
    total = p.sum(-1, keepdims=True) + 1.0
    w = p * pick(f64(vs))[:, :1, :]
    y = mxq(w, 2, "e4m3") @ mxq(pick(v).transpose(0, 2, 1), 1, "e4m3")
    y = y / total
    return y

@@ -1,0 +1,221 @@
+from contextlib import ExitStack
+
+import concourse.mybir as mybir
+from concourse.masks import make_identity
+
+F32 = mybir.dt.float32
+BF16 = mybir.dt.bfloat16
+I32 = mybir.dt.int32
+U32 = mybir.dt.uint32
+U16 = mybir.dt.uint16
+U8 = mybir.dt.uint8
+FP8X4 = mybir.dt.float8_e4m3fn_x4
+FP4X4 = mybir.dt.float4_e2m1fn_x4
+ACT = mybir.ActivationFunctionType
+ALU = mybir.AluOpType
+
+P = 128
+PACK = 4
+RUN = 8
+N, T, D, DV, NQ = 512, 1024, 1024, 256, 256
+PASSES = D // (P * PACK)
+HALVES = NQ // P
+CAP = 2.0
+
+FLOPS = 2 * NQ * N * (D + DV)
+
+
+def by_place(ap):
+    return ap.rearrange("p (t b j) -> p b t j", t=PACK, j=RUN)
+
+
+def tile_attend_rel2_cap_topkq256n512t1024_kernel(tc, qT, k_words, k_scales, vT, vs, offs, out):
+    nc = tc.nc
+    with ExitStack() as ctx:
+        sb = ctx.enter_context(tc.tile_pool(name="sb", bufs=1))
+        ps = ctx.enter_context(tc.psum_pool(name="ps", bufs=1))
+
+        offsets = sb.tile([P, N // 16], U16, name="offsets")
+        nc.sync.dma_start(offsets[:], offs)
+
+        ks_pool = sb.tile([P, T // 4], I32, name="ks_pool", tag="keys", align_bytes=64)
+        nc.vector.memset(ks_pool[:], 0)
+        ks_rows = k_scales.bitcast(I32).rearrange("o (g f) t -> f g o t", f=4)
+        for f in range(4):
+            nc.sync.dma_start(ks_pool[f:P:16, :], ks_rows[f])
+
+        kw_pool = sb.tile([P, T], I32, name="kw_pool", align_bytes=64)
+        nc.scalar.dma_start(kw_pool[:], k_words[0].rearrange("p t b -> p (t b)").bitcast(I32))
+        q_raw = [sb.tile([P, PACK, NQ], F32, name=f"q_raw{o}", align_bytes=64) for o in range(PASSES)]
+        for o in range(PASSES):
+            rows = qT[0, o * P * PACK : (o + 1) * P * PACK, :]
+            nc.scalar.dma_start(q_raw[o][:], rows.rearrange("(p t) q -> p t q", t=PACK))
+
+        table_in = sb.tile([P, 1], F32, name="table_in", tag="half1", align_bytes=64)
+        table_out = sb.tile([P, 1], F32, name="table_out", tag="half0", align_bytes=64)
+        nc.gpsimd.memset(table_in[:], 0.0)
+        nc.scalar.activation(table_out[:], table_in[:], ACT.Tanh)
+
+        vs_pool = sb.tile([P, T], F32, name="vs_pool", align_bytes=64)
+        nc.vector.memset(vs_pool[:], 0.0)
+        nc.gpsimd.dma_start(vs_pool[0:1, :], vs[0:1, :])
+        ks_second = sb.tile([P, N // 4], I32, name="ks_second", align_bytes=64)
+        nc.vector.memset(ks_second[:], 0)
+        ident = sb.tile([P, P], F32, name="ident", align_bytes=64)
+        make_identity(nc, ident[:])
+
+        v_rows = vT.rearrange("(f u) t -> f u t", u=2)
+        v_raw = [sb.tile([P, 2, T // 2], F32, name=f"v_raw{c}", tag=f"half{c}", align_bytes=64) for c in range(2)]
+        for c in range(2):
+            nc.scalar.dma_start(v_raw[c][:], v_rows[:, :, c * (T // 2) : (c + 1) * (T // 2)])
+
+        ks_got = sb.tile([P, N], U8, name="ks_got", align_bytes=64)
+        nc.vector.tensor_copy(ks_got[:], ks_pool[:].bitcast(U8).indirect(offsets[:]))
+        ks_first = sb.tile([P, N // 4], I32, name="ks_first", align_bytes=64)
+        nc.vector.tensor_copy(
+            ks_first[:].rearrange("p (t b w) -> p t b w", t=PACK, w=RUN // 4),
+            ks_got[:].bitcast(I32).rearrange("p (b t w) -> p t b w", t=PACK, w=RUN // 4),
+        )
+        nc.sync.dma_start(ks_second[0:112, :], ks_first[16:128, :])
+        k_planes = [ks_first[:].bitcast(U8), ks_second[:].bitcast(U8)]
+        kw_got = sb.tile([P, N], U32, name="kw_got", tag="keys", align_bytes=64)
+        nc.vector.tensor_copy(kw_got[:], kw_pool[:].bitcast(U32).indirect(offsets[:]))
+        k_codes = sb.tile([P, PASSES, N], U16, name="k_codes", align_bytes=64)
+        nc.vector.tensor_copy(
+            k_codes[:].rearrange("p o (t b j) -> p o t b j", t=PACK, j=RUN),
+            kw_got[:].bitcast(U16).rearrange("p (b t j o) -> p o t b j", t=PACK, j=RUN, o=PASSES),
+        )
+
+        q_codes = sb.tile([P, HALVES, PASSES, P], U32, name="q_codes", align_bytes=64)
+        q_scales = sb.tile([P, HALVES, PASSES, P], U8, name="q_scales", align_bytes=64)
+        q_bf = sb.tile([P, HALVES, PASSES, P, PACK], BF16, name="q_bf", tag="q_bf", align_bytes=64)
+        for o in range(PASSES):
+            for h in range(HALVES):
+                nc.scalar.activation(
+                    q_bf[:, h, o].rearrange("p (c i) t -> p c t i", i=4),
+                    q_raw[o][:, :, h * P : (h + 1) * P].rearrange("p t (c i) -> p c t i", i=4),
+                    ACT.Copy,
+                )
+        for h in range(HALVES):
+            nc.vector.quantize_mx(
+                out=q_codes[:, h].rearrange("p o q -> p (o q)").bitcast(FP8X4),
+                scales=q_scales[:, h].rearrange("p o q -> p (o q)"),
+                in_=q_bf[:, h].rearrange("p o q t -> p (o q t)"),
+            )
+
+        scores = [[ps.tile([P, 2, P], F32, name=f"scores{h}{c}", tag=f"bank{h}{c}") for c in range(2)] for h in range(HALVES)]
+        for h in range(HALVES):
+            for t in range(PACK):
+                k_cols = slice(t * P, (t + 1) * P)
+                for o in range(PASSES):
+                    nc.tensor.matmul_mx(
+                        out=scores[h][t // 2][:, t % 2, :],
+                        lhsT=k_codes[:, o, k_cols].bitcast(FP4X4),
+                        lhsT_scale=k_planes[o][:, k_cols],
+                        rhs=q_codes[:, h, o, :].bitcast(FP8X4),
+                        rhs_scale=q_scales[:, h, o, :],
+                        start=(o == 0),
+                        stop=(o == PASSES - 1),
+                    )
+
+        v_pool = sb.tile([P, T, 2], BF16, name="v_pool", align_bytes=64)
+        for c in range(2):
+            nc.scalar.activation(
+                v_pool[:, c * (T // 2) : (c + 1) * (T // 2), :],
+                v_raw[c][:].rearrange("p u t -> p t u"),
+                ACT.Copy,
+            )
+        vs_got = sb.tile([P, N], U32, name="vs_got", tag="q_bf", align_bytes=64)
+        nc.vector.tensor_copy(by_place(vs_got[:]), vs_pool[:].bitcast(U32).indirect(offsets[:]))
+        v_got = sb.tile([P, N], U32, name="v_got", align_bytes=64)
+        nc.vector.tensor_copy(
+            by_place(v_got[:]),
+            v_pool[:].rearrange("p t u -> p (t u)").bitcast(U32).indirect(offsets[:]),
+        )
+
+        th = [sb.tile([P, PACK, P], F32, name=f"th{h}", tag=f"half{h}", align_bytes=64) for h in range(HALVES)]
+        for h in range(HALVES):
+            for c in range(2):
+                nc.scalar.activation(th[h][:, 2 * c : 2 * c + 2, :], scores[h][c][:], ACT.Tanh, scale=1.0 / CAP)
+
+        vs_turned = ps.tile([P, PACK, P], F32, name="vs_turned")
+        v_turned = ps.tile([P, PACK, P], F32, name="v_turned")
+        for t in range(PACK):
+            nc.tensor.transpose(vs_turned[:, t, :], vs_got[:, t * P : (t + 1) * P].bitcast(F32), ident[:])
+        for t in range(PACK):
+            nc.tensor.transpose(v_turned[:, t, :], v_got[:, t * P : (t + 1) * P].bitcast(F32), ident[:])
+        v_bf = sb.tile([P, DV, PACK], BF16, name="v_bf", align_bytes=64)
+        nc.scalar.copy(v_bf[:], v_turned[:].bitcast(BF16).rearrange("p t e -> p e t"))
+
+        pq = [sb.tile([P, PACK, P], F32, name=f"pq{h}", align_bytes=64) for h in range(HALVES)]
+        for h in range(HALVES):
+            for c in range(2):
+                pair = slice(2 * c, 2 * c + 2)
+                nc.vector.scalar_tensor_tensor(
+                    out=pq[h][:, pair, :],
+                    in0=th[h][:, pair, :],
+                    scalar=0.0,
+                    in1=th[h][:, pair, :],
+                    op0=ALU.max,
+                    op1=ALU.mult,
+                )
+        p_turned = [ps.tile([P, PACK, P], F32, name=f"p_turned{h}") for h in range(HALVES)]
+        sums = sb.tile([P, HALVES], F32, name="sums")
+        spill = sb.tile([P, PACK, P], BF16, name="spill")
+        for h in range(HALVES):
+            for t in range(PACK):
+                nc.tensor.transpose(p_turned[h][:, t, :], pq[h][:, t, :], ident[:])
+            nc.scalar.activation(
+                spill[:], p_turned[h][:], ACT.Copy, bias=1.0 / (CAP * CAP * N), accum_out=sums[:, h : h + 1]
+            )
+
+        v_codes = sb.tile([P, DV], U32, name="v_codes", align_bytes=64)
+        v_scales = sb.tile([P, DV], U8, name="v_scales", align_bytes=64)
+        w_bf = [sb.tile([P, P, PACK], BF16, name=f"w_bf{h}", align_bytes=64) for h in range(HALVES)]
+        w_codes = [sb.tile([P, P], U32, name=f"w_codes{h}", align_bytes=64) for h in range(HALVES)]
+        w_scales = [sb.tile([P, P], U8, name=f"w_scales{h}", align_bytes=64) for h in range(HALVES)]
+        vs_cols = vs_turned[:, :, 0:1].unsqueeze(1).broadcast_to([P, P // 4, PACK, 4])
+
+        def weigh(h):
+            nc.vector.tensor_tensor(
+                out=w_bf[h][:].rearrange("p (c i) t -> p c t i", i=4),
+                in0=pq[h][:].rearrange("p t (c i) -> p c t i", i=4),
+                in1=vs_cols,
+                op=ALU.mult,
+            )
+
+        def quantise_w(h):
+            nc.vector.quantize_mx(
+                out=w_codes[h][:].bitcast(FP8X4),
+                scales=w_scales[h][:],
+                in_=w_bf[h][:].rearrange("p q t -> p (q t)"),
+            )
+
+        inverse = sb.tile([P, HALVES], F32, name="inverse")
+        weigh(0)
+        nc.vector.quantize_mx(
+            out=v_codes[:].bitcast(FP8X4), scales=v_scales[:], in_=v_bf[:].rearrange("p e t -> p (e t)")
+        )
+        quantise_w(0)
+        weigh(1)
+        nc.vector.reciprocal(inverse[:, 0:1], sums[:, 0:1])
+        quantise_w(1)
+        nc.vector.reciprocal(inverse[:, 1:2], sums[:, 1:2])
+
+        for h in range(HALVES):
+            acc = ps.tile([P, DV], F32, name=f"acc{h}", tag=f"bank0{h}")
+            nc.tensor.matmul_mx(
+                out=acc[:],
+                lhsT=w_codes[h][:].bitcast(FP8X4),
+                lhsT_scale=w_scales[h][:],
+                rhs=v_codes[:].bitcast(FP8X4),
+                rhs_scale=v_scales[:],
+                start=True,
+                stop=True,
+            )
+            y = sb.tile([P, DV], F32, name=f"y{h}", align_bytes=64)
+            if h == 0:
+                nc.scalar.activation(y[:], acc[:], ACT.Copy, scale=inverse[:, h : h + 1])
+            else:
+                nc.vector.tensor_scalar(y[:], acc[:], inverse[:, h : h + 1], None, ALU.mult)
+            nc.sync.dma_start(out[0, h * P : (h + 1) * P, :], y[:])

@@ -36,6 +36,11 @@ def tile_attend_rel2_cap_topkq256n512t1024_kernel(tc, qT, k_words, k_scales, vT,
         ps = ctx.enter_context(tc.psum_pool(name="ps", bufs=1))
 
         offsets = sb.tile([P, N // 16], U16, name="offsets")
+        kw_pool = sb.tile([P, T], I32, name="kw_pool", align_bytes=64)
+        kw_rows = k_words[0].rearrange("p t b -> p (t b)").bitcast(I32)
+        for c in range(2):
+            cols = slice(c * (T // 2), (c + 1) * (T // 2))
+            nc.sync.dma_start(kw_pool[:, cols], kw_rows[:, cols])
         nc.sync.dma_start(offsets[:], offs)
 
         ks_pool = sb.tile([P, T // 4], I32, name="ks_pool", tag="keys", align_bytes=64)
@@ -44,39 +49,43 @@ def tile_attend_rel2_cap_topkq256n512t1024_kernel(tc, qT, k_words, k_scales, vT,
         for f in range(4):
             nc.sync.dma_start(ks_pool[f:P:16, :], ks_rows[f])
 
-        kw_pool = sb.tile([P, T], I32, name="kw_pool", align_bytes=64)
-        nc.scalar.dma_start(kw_pool[:], k_words[0].rearrange("p t b -> p (t b)").bitcast(I32))
         q_raw = [sb.tile([P, PACK, NQ], F32, name=f"q_raw{o}", align_bytes=64) for o in range(PASSES)]
         for o in range(PASSES):
             rows = qT[0, o * P * PACK : (o + 1) * P * PACK, :]
-            nc.scalar.dma_start(q_raw[o][:], rows.rearrange("(p t) q -> p t q", t=PACK))
+            nc.sync.dma_start(q_raw[o][:], rows.rearrange("(p t) q -> p t q", t=PACK))
 
-        table_in = sb.tile([P, 1], F32, name="table_in", tag="half1", align_bytes=64)
-        table_out = sb.tile([P, 1], F32, name="table_out", tag="half0", align_bytes=64)
+        table_in = sb.tile([P, 1], F32, name="table_in")
+        table_out = sb.tile([P, 1], F32, name="table_out")
         nc.gpsimd.memset(table_in[:], 0.0)
         nc.scalar.activation(table_out[:], table_in[:], ACT.Tanh)
 
         vs_pool = sb.tile([P, T], F32, name="vs_pool", align_bytes=64)
         nc.vector.memset(vs_pool[:], 0.0)
-        nc.gpsimd.dma_start(vs_pool[0:1, :], vs[0:1, :])
+        nc.sync.dma_start(vs_pool[0:1, :], vs[0:1, :])
         ks_second = sb.tile([P, N // 4], I32, name="ks_second", align_bytes=64)
         nc.vector.memset(ks_second[:], 0)
         ident = sb.tile([P, P], F32, name="ident", align_bytes=64)
         make_identity(nc, ident[:])
 
         v_rows = vT.rearrange("(f u) t -> f u t", u=2)
-        v_raw = [sb.tile([P, 2, T // 2], F32, name=f"v_raw{c}", tag=f"half{c}", align_bytes=64) for c in range(2)]
-        for c in range(2):
-            nc.scalar.dma_start(v_raw[c][:], v_rows[:, :, c * (T // 2) : (c + 1) * (T // 2)])
+        v_cuts = [0, T // 2, 3 * T // 4, T]
+        v_raw = []
+        for c, tag in enumerate(("half0", "half1")):
+            piece = sb.tile([P, 2, v_cuts[c + 1] - v_cuts[c]], F32, name=f"v_raw{c}", tag=tag, align_bytes=64)
+            nc.sync.dma_start(piece[:], v_rows[:, :, v_cuts[c] : v_cuts[c + 1]])
+            v_raw.append(piece)
 
-        ks_got = sb.tile([P, N], U8, name="ks_got", align_bytes=64)
+        ks_got = sb.tile([P, N], U8, name="ks_got", tag="late", align_bytes=64)
         nc.vector.tensor_copy(ks_got[:], ks_pool[:].bitcast(U8).indirect(offsets[:]))
         ks_first = sb.tile([P, N // 4], I32, name="ks_first", align_bytes=64)
         nc.vector.tensor_copy(
             ks_first[:].rearrange("p (t b w) -> p t b w", t=PACK, w=RUN // 4),
             ks_got[:].bitcast(I32).rearrange("p (b t w) -> p t b w", t=PACK, w=RUN // 4),
         )
-        nc.sync.dma_start(ks_second[0:112, :], ks_first[16:128, :])
+        for lo, hi in ((0, 64), (64, 96), (96, 112)):
+            nc.sync.dma_start(ks_second[lo:hi, :], ks_first[lo + 16 : hi + 16, :])
+        v_late = sb.tile([P, 2, T // 4], F32, name="v_late", tag="late", align_bytes=64)
+        nc.sync.dma_start(v_late[:], v_rows[:, :, v_cuts[2] :])
         k_planes = [ks_first[:].bitcast(U8), ks_second[:].bitcast(U8)]
         kw_got = sb.tile([P, N], U32, name="kw_got", tag="keys", align_bytes=64)
         nc.vector.tensor_copy(kw_got[:], kw_pool[:].bitcast(U32).indirect(offsets[:]))
@@ -121,12 +130,13 @@ def tile_attend_rel2_cap_topkq256n512t1024_kernel(tc, qT, k_words, k_scales, vT,
         v_pool = sb.tile([P, T, 2], BF16, name="v_pool", align_bytes=64)
         for c in range(2):
             nc.scalar.activation(
-                v_pool[:, c * (T // 2) : (c + 1) * (T // 2), :],
+                v_pool[:, v_cuts[c] : v_cuts[c + 1], :],
                 v_raw[c][:].rearrange("p u t -> p t u"),
                 ACT.Copy,
             )
         vs_got = sb.tile([P, N], U32, name="vs_got", tag="q_bf", align_bytes=64)
         nc.vector.tensor_copy(by_place(vs_got[:]), vs_pool[:].bitcast(U32).indirect(offsets[:]))
+        nc.vector.tensor_copy(v_pool[:, v_cuts[2] :, :], v_late[:].rearrange("p u t -> p t u"))
         v_got = sb.tile([P, N], U32, name="v_got", align_bytes=64)
         nc.vector.tensor_copy(
             by_place(v_got[:]),

@@ -36,33 +36,31 @@ def tile_attend_rel2_cap_topkq256n512t1024_kernel(tc, qT, k_words, k_scales, vT,
         ps = ctx.enter_context(tc.psum_pool(name="ps", bufs=1))
 
         offsets = sb.tile([P, N // 16], U16, name="offsets")
-        kw_pool = sb.tile([P, T], I32, name="kw_pool", align_bytes=64)
+        kw_pool = sb.tile([P, T], I32, name="kw_pool", tag="kw_pool", align_bytes=64)
         kw_rows = k_words[0].rearrange("p t b -> p (t b)").bitcast(I32)
-        for c in range(2):
-            cols = slice(c * (T // 2), (c + 1) * (T // 2))
-            nc.sync.dma_start(kw_pool[:, cols], kw_rows[:, cols])
+        q_raw = [sb.tile([P, PACK, NQ], F32, name=f"q_raw{o}", tag=f"q_raw{o}", align_bytes=64) for o in range(PASSES)]
+        q_rows = qT[0].rearrange("(o p t) q -> o p t q", p=P, t=PACK)
+        nc.sync.dma_start(q_raw[0][:], q_rows[0])
         nc.sync.dma_start(offsets[:], offs)
 
-        ks_pool = sb.tile([P, T // 4], I32, name="ks_pool", tag="keys", align_bytes=64)
+        ks_pool = sb.tile([P, T // 4], I32, name="ks_pool", tag="late", align_bytes=64)
         nc.vector.memset(ks_pool[:], 0)
         ks_rows = k_scales.bitcast(I32).rearrange("o (g f) t -> f g o t", f=4)
         for f in range(4):
             nc.sync.dma_start(ks_pool[f:P:16, :], ks_rows[f])
 
-        q_raw = [sb.tile([P, PACK, NQ], F32, name=f"q_raw{o}", align_bytes=64) for o in range(PASSES)]
-        for o in range(PASSES):
-            rows = qT[0, o * P * PACK : (o + 1) * P * PACK, :]
-            nc.sync.dma_start(q_raw[o][:], rows.rearrange("(p t) q -> p t q", t=PACK))
+        nc.sync.dma_start(kw_pool[:], kw_rows)
+        nc.sync.dma_start(q_raw[1][:], q_rows[1])
 
         table_in = sb.tile([P, 1], F32, name="table_in")
         table_out = sb.tile([P, 1], F32, name="table_out")
         nc.gpsimd.memset(table_in[:], 0.0)
         nc.scalar.activation(table_out[:], table_in[:], ACT.Tanh)
 
-        vs_pool = sb.tile([P, T], F32, name="vs_pool", align_bytes=64)
+        vs_pool = sb.tile([P, T], F32, name="vs_pool", tag="vs_pool", align_bytes=64)
         nc.vector.memset(vs_pool[:], 0.0)
         nc.sync.dma_start(vs_pool[0:1, :], vs[0:1, :])
-        ks_second = sb.tile([P, N // 4], I32, name="ks_second", align_bytes=64)
+        ks_second = sb.tile([P, N // 4], I32, name="ks_second", tag="ks_second", align_bytes=64)
         nc.vector.memset(ks_second[:], 0)
         ident = sb.tile([P, P], F32, name="ident", align_bytes=64)
         make_identity(nc, ident[:])
@@ -75,19 +73,25 @@ def tile_attend_rel2_cap_topkq256n512t1024_kernel(tc, qT, k_words, k_scales, vT,
             nc.sync.dma_start(piece[:], v_rows[:, :, v_cuts[c] : v_cuts[c + 1]])
             v_raw.append(piece)
 
-        ks_got = sb.tile([P, N], U8, name="ks_got", tag="late", align_bytes=64)
+        warm = [ps.tile([P, PACK, P], F32, name=f"warm{h}", tag=f"acc{h}") for h in range(HALVES)]
+        sources = [ident[:]] * 12 + [q_raw[0][:, 0, :P]] * 14 + [q_raw[1][:, 0, :P]] * 7
+        for n, source in enumerate(sources):
+            nc.tensor.transpose(warm[n // PACK % 2][:, n % PACK, :], source, ident[:])
+
+        def lay_by_place(plane, listed):
+            nc.vector.tensor_copy(
+                plane[:].rearrange("p (t b w) -> p t b w", t=PACK, w=RUN // 4),
+                listed.rearrange("p (b t w) -> p t b w", t=PACK, w=RUN // 4),
+            )
+
+        ks_got = sb.tile([P, N], U8, name="ks_got", align_bytes=64)
         nc.vector.tensor_copy(ks_got[:], ks_pool[:].bitcast(U8).indirect(offsets[:]))
-        ks_first = sb.tile([P, N // 4], I32, name="ks_first", align_bytes=64)
-        nc.vector.tensor_copy(
-            ks_first[:].rearrange("p (t b w) -> p t b w", t=PACK, w=RUN // 4),
-            ks_got[:].bitcast(I32).rearrange("p (b t w) -> p t b w", t=PACK, w=RUN // 4),
-        )
         for lo, hi in ((0, 64), (64, 96), (96, 112)):
-            nc.sync.dma_start(ks_second[lo:hi, :], ks_first[lo + 16 : hi + 16, :])
+            nc.sync.dma_start(ks_second[lo:hi, :], ks_got[lo + 16 : hi + 16, :].bitcast(I32))
         v_late = sb.tile([P, 2, T // 4], F32, name="v_late", tag="late", align_bytes=64)
         nc.sync.dma_start(v_late[:], v_rows[:, :, v_cuts[2] :])
-        k_planes = [ks_first[:].bitcast(U8), ks_second[:].bitcast(U8)]
-        kw_got = sb.tile([P, N], U32, name="kw_got", tag="keys", align_bytes=64)
+        v_raw.append(v_late)
+        kw_got = sb.tile([P, N], U32, name="kw_got", align_bytes=64)
         nc.vector.tensor_copy(kw_got[:], kw_pool[:].bitcast(U32).indirect(offsets[:]))
         k_codes = sb.tile([P, PASSES, N], U16, name="k_codes", align_bytes=64)
         nc.vector.tensor_copy(
@@ -97,86 +101,97 @@ def tile_attend_rel2_cap_topkq256n512t1024_kernel(tc, qT, k_words, k_scales, vT,
 
         q_codes = sb.tile([P, HALVES, PASSES, P], U32, name="q_codes", align_bytes=64)
         q_scales = sb.tile([P, HALVES, PASSES, P], U8, name="q_scales", align_bytes=64)
-        q_bf = sb.tile([P, HALVES, PASSES, P, PACK], BF16, name="q_bf", tag="q_bf", align_bytes=64)
+        q_bf = [sb.tile([P, PASSES, P, PACK], BF16, name=f"q_bf{h}", tag=f"q_bf{h}", align_bytes=64) for h in range(HALVES)]
         for o in range(PASSES):
             for h in range(HALVES):
                 nc.scalar.activation(
-                    q_bf[:, h, o].rearrange("p (c i) t -> p c t i", i=4),
+                    q_bf[h][:, o].rearrange("p (c i) t -> p c t i", i=4),
                     q_raw[o][:, :, h * P : (h + 1) * P].rearrange("p t (c i) -> p c t i", i=4),
                     ACT.Copy,
                 )
+        plane0 = sb.tile([P, N // 4], I32, name="plane0", tag="q_raw1", align_bytes=64)
+        lay_by_place(plane0, ks_got[:].bitcast(I32))
         for h in range(HALVES):
             nc.vector.quantize_mx(
                 out=q_codes[:, h].rearrange("p o q -> p (o q)").bitcast(FP8X4),
                 scales=q_scales[:, h].rearrange("p o q -> p (o q)"),
-                in_=q_bf[:, h].rearrange("p o q t -> p (o q t)"),
+                in_=q_bf[h][:].rearrange("p o q t -> p (o q t)"),
             )
+
+        plane1 = sb.tile([P, N // 4], I32, name="plane1", tag="q_bf0", align_bytes=64)
+        lay_by_place(plane1, ks_second[:])
+        k_planes = [plane0[:].bitcast(U8), plane1[:].bitcast(U8)]
 
         scores = [[ps.tile([P, 2, P], F32, name=f"scores{h}{c}", tag=f"bank{h}{c}") for c in range(2)] for h in range(HALVES)]
-        for h in range(HALVES):
-            for t in range(PACK):
-                k_cols = slice(t * P, (t + 1) * P)
-                for o in range(PASSES):
-                    nc.tensor.matmul_mx(
-                        out=scores[h][t // 2][:, t % 2, :],
-                        lhsT=k_codes[:, o, k_cols].bitcast(FP4X4),
-                        lhsT_scale=k_planes[o][:, k_cols],
-                        rhs=q_codes[:, h, o, :].bitcast(FP8X4),
-                        rhs_scale=q_scales[:, h, o, :],
-                        start=(o == 0),
-                        stop=(o == PASSES - 1),
-                    )
-
-        v_pool = sb.tile([P, T, 2], BF16, name="v_pool", align_bytes=64)
-        for c in range(2):
-            nc.scalar.activation(
-                v_pool[:, v_cuts[c] : v_cuts[c + 1], :],
-                v_raw[c][:].rearrange("p u t -> p t u"),
-                ACT.Copy,
+        every = [(h, t, o) for h in range(HALVES) for t in range(PACK) for o in range(PASSES)]
+        opening = [(h, t, o) for h, t, o in every if t % 2 == 0 and o == 0]
+        for h, t, o in opening + [x for x in every if x not in opening]:
+            k_cols = slice(t * P, (t + 1) * P)
+            nc.tensor.matmul_mx(
+                out=scores[h][t // 2][:, t % 2, :],
+                lhsT=k_codes[:, o, k_cols].bitcast(FP4X4),
+                lhsT_scale=k_planes[o][:, k_cols],
+                rhs=q_codes[:, h, o, :].bitcast(FP8X4),
+                rhs_scale=q_scales[:, h, o, :],
+                start=(o == 0),
+                stop=(o == PASSES - 1),
             )
-        vs_got = sb.tile([P, N], U32, name="vs_got", tag="q_bf", align_bytes=64)
+
+        v_pool = sb.tile([P, T, 2], BF16, name="v_pool", tag="v_pool", align_bytes=64)
+        for c in range(3):
+            place = v_pool[:, v_cuts[c] : v_cuts[c + 1], :]
+            piece = v_raw[c][:].rearrange("p u t -> p t u")
+            if c == 1:
+                nc.vector.tensor_copy(place, piece)
+            else:
+                nc.scalar.activation(place, piece, ACT.Copy)
+        vs_got = sb.tile([P, N], U32, name="vs_got", tag="ks_second", align_bytes=64)
         nc.vector.tensor_copy(by_place(vs_got[:]), vs_pool[:].bitcast(U32).indirect(offsets[:]))
-        nc.vector.tensor_copy(v_pool[:, v_cuts[2] :, :], v_late[:].rearrange("p u t -> p t u"))
         v_got = sb.tile([P, N], U32, name="v_got", align_bytes=64)
         nc.vector.tensor_copy(
             by_place(v_got[:]),
             v_pool[:].rearrange("p t u -> p (t u)").bitcast(U32).indirect(offsets[:]),
         )
 
-        th = [sb.tile([P, PACK, P], F32, name=f"th{h}", tag=f"half{h}", align_bytes=64) for h in range(HALVES)]
+        th = [
+            sb.tile([P, PACK, P], F32, name="th0", tag="late", align_bytes=64),
+            sb.tile([P, PACK, P], F32, name="th1", align_bytes=64),
+        ]
         for h in range(HALVES):
             for c in range(2):
                 nc.scalar.activation(th[h][:, 2 * c : 2 * c + 2, :], scores[h][c][:], ACT.Tanh, scale=1.0 / CAP)
 
-        vs_turned = ps.tile([P, PACK, P], F32, name="vs_turned")
-        v_turned = ps.tile([P, PACK, P], F32, name="v_turned")
+        vs_turned = ps.tile([P, PACK, P], F32, name="vs_turned", tag="bank00")
+        v_turned = ps.tile([P, PACK, P], F32, name="v_turned", tag="bank01")
         for t in range(PACK):
             nc.tensor.transpose(vs_turned[:, t, :], vs_got[:, t * P : (t + 1) * P].bitcast(F32), ident[:])
         for t in range(PACK):
             nc.tensor.transpose(v_turned[:, t, :], v_got[:, t * P : (t + 1) * P].bitcast(F32), ident[:])
-        v_bf = sb.tile([P, DV, PACK], BF16, name="v_bf", align_bytes=64)
-        nc.scalar.copy(v_bf[:], v_turned[:].bitcast(BF16).rearrange("p t e -> p e t"))
-
         pq = [sb.tile([P, PACK, P], F32, name=f"pq{h}", align_bytes=64) for h in range(HALVES)]
-        for h in range(HALVES):
-            for c in range(2):
-                pair = slice(2 * c, 2 * c + 2)
-                nc.vector.scalar_tensor_tensor(
-                    out=pq[h][:, pair, :],
-                    in0=th[h][:, pair, :],
-                    scalar=0.0,
-                    in1=th[h][:, pair, :],
-                    op0=ALU.max,
-                    op1=ALU.mult,
-                )
-        p_turned = [ps.tile([P, PACK, P], F32, name=f"p_turned{h}") for h in range(HALVES)]
+        positive = sb.tile([P, PACK, P], F32, name="positive", align_bytes=64)
+        pairs = [slice(0, 2), slice(2, 4)]
+        nc.vector.scalar_tensor_tensor(
+            out=pq[0][:], in0=th[0][:], scalar=0.0, in1=th[0][:], op0=ALU.max, op1=ALU.mult
+        )
+        for pair in pairs:
+            nc.scalar.activation(positive[:, pair, :], th[1][:, pair, :], ACT.Relu)
+        for pair in pairs:
+            nc.scalar.activation(pq[1][:, pair, :], positive[:, pair, :], ACT.Square)
+        v_bf = sb.tile([P, DV, PACK], BF16, name="v_bf", align_bytes=64)
+        v_pairs = v_turned[:].bitcast(BF16).rearrange("p t e -> p e t")
+        e_halves = [slice(0, P), slice(P, DV)]
+        for cols in e_halves:
+            nc.scalar.copy(v_bf[:, cols, :], v_pairs[:, cols, :])
         sums = sb.tile([P, HALVES], F32, name="sums")
-        spill = sb.tile([P, PACK, P], BF16, name="spill")
+        spill = sb.tile([P, P], BF16, name="spill")
         for h in range(HALVES):
+            p_turned = ps.tile([P, P], F32, name=f"p_turned{h}")
             for t in range(PACK):
-                nc.tensor.transpose(p_turned[h][:, t, :], pq[h][:, t, :], ident[:])
+                nc.tensor.matmul(
+                    p_turned[:], pq[h][:, t, :], ident[:], start=(t == 0), stop=(t == PACK - 1), is_transpose=True
+                )
             nc.scalar.activation(
-                spill[:], p_turned[h][:], ACT.Copy, bias=1.0 / (CAP * CAP * N), accum_out=sums[:, h : h + 1]
+                spill[:], p_turned[:], ACT.Copy, bias=1.0 / (CAP * CAP * P), accum_out=sums[:, h : h + 1]
             )
 
         v_codes = sb.tile([P, DV], U32, name="v_codes", align_bytes=64)
@@ -185,47 +200,44 @@ def tile_attend_rel2_cap_topkq256n512t1024_kernel(tc, qT, k_words, k_scales, vT,
         w_codes = [sb.tile([P, P], U32, name=f"w_codes{h}", align_bytes=64) for h in range(HALVES)]
         w_scales = [sb.tile([P, P], U8, name=f"w_scales{h}", align_bytes=64) for h in range(HALVES)]
         vs_cols = vs_turned[:, :, 0:1].unsqueeze(1).broadcast_to([P, P // 4, PACK, 4])
-
-        def weigh(h):
+        for h in range(HALVES):
             nc.vector.tensor_tensor(
                 out=w_bf[h][:].rearrange("p (c i) t -> p c t i", i=4),
                 in0=pq[h][:].rearrange("p t (c i) -> p c t i", i=4),
                 in1=vs_cols,
                 op=ALU.mult,
             )
-
-        def quantise_w(h):
+        for h in range(HALVES):
             nc.vector.quantize_mx(
                 out=w_codes[h][:].bitcast(FP8X4),
                 scales=w_scales[h][:],
                 in_=w_bf[h][:].rearrange("p q t -> p (q t)"),
             )
-
-        inverse = sb.tile([P, HALVES], F32, name="inverse")
-        weigh(0)
-        nc.vector.quantize_mx(
-            out=v_codes[:].bitcast(FP8X4), scales=v_scales[:], in_=v_bf[:].rearrange("p e t -> p (e t)")
-        )
-        quantise_w(0)
-        weigh(1)
-        nc.vector.reciprocal(inverse[:, 0:1], sums[:, 0:1])
-        quantise_w(1)
-        nc.vector.reciprocal(inverse[:, 1:2], sums[:, 1:2])
-
-        for h in range(HALVES):
-            acc = ps.tile([P, DV], F32, name=f"acc{h}", tag=f"bank0{h}")
-            nc.tensor.matmul_mx(
-                out=acc[:],
-                lhsT=w_codes[h][:].bitcast(FP8X4),
-                lhsT_scale=w_scales[h][:],
-                rhs=v_codes[:].bitcast(FP8X4),
-                rhs_scale=v_scales[:],
-                start=True,
-                stop=True,
+            nc.vector.quantize_mx(
+                out=v_codes[:, e_halves[h]].bitcast(FP8X4),
+                scales=v_scales[:, e_halves[h]],
+                in_=v_bf[:, e_halves[h], :].rearrange("p e t -> p (e t)"),
             )
+        inverse = sb.tile([P, HALVES], F32, name="inverse")
+        nc.vector.reciprocal(inverse[:], sums[:])
+
+        acc = [ps.tile([P, DV], F32, name=f"acc{h}", tag=f"acc{h}") for h in range(HALVES)]
+        for cols in e_halves:
+            for h in range(HALVES):
+                nc.tensor.matmul_mx(
+                    out=acc[h][:, cols],
+                    lhsT=w_codes[h][:].bitcast(FP8X4),
+                    lhsT_scale=w_scales[h][:],
+                    rhs=v_codes[:, cols].bitcast(FP8X4),
+                    rhs_scale=v_scales[:, cols],
+                    start=True,
+                    stop=True,
+                )
+        for h in range(HALVES):
             y = sb.tile([P, DV], F32, name=f"y{h}", align_bytes=64)
             if h == 0:
-                nc.scalar.activation(y[:], acc[:], ACT.Copy, scale=inverse[:, h : h + 1])
+                nc.scalar.activation(y[:], acc[h][:], ACT.Copy, scale=inverse[:, h : h + 1])
+                nc.scalar.dma_start(out[0, h * P : (h + 1) * P, :], y[:])
             else:
-                nc.vector.tensor_scalar(y[:], acc[:], inverse[:, h : h + 1], None, ALU.mult)
-            nc.sync.dma_start(out[0, h * P : (h + 1) * P, :], y[:])
+                nc.vector.tensor_scalar(y[:], acc[h][:], inverse[:, h : h + 1], None, ALU.mult)
+                nc.sync.dma_start(out[0, h * P : (h + 1) * P, :], y[:])

@@ -73,11 +73,6 @@ def tile_attend_rel2_cap_topkq256n512t1024_kernel(tc, qT, k_words, k_scales, vT,
             nc.sync.dma_start(piece[:], v_rows[:, :, v_cuts[c] : v_cuts[c + 1]])
             v_raw.append(piece)
 
-        warm = [ps.tile([P, PACK, P], F32, name=f"warm{h}", tag=f"acc{h}") for h in range(HALVES)]
-        sources = [ident[:]] * 12 + [q_raw[0][:, 0, :P]] * 14 + [q_raw[1][:, 0, :P]] * 7
-        for n, source in enumerate(sources):
-            nc.tensor.transpose(warm[n // PACK % 2][:, n % PACK, :], source, ident[:])
-
         def lay_by_place(plane, listed):
             nc.vector.tensor_copy(
                 plane[:].rearrange("p (t b w) -> p t b w", t=PACK, w=RUN // 4),
@@ -221,7 +216,7 @@ def tile_attend_rel2_cap_topkq256n512t1024_kernel(tc, qT, k_words, k_scales, vT,
         inverse = sb.tile([P, HALVES], F32, name="inverse")
         nc.vector.reciprocal(inverse[:], sums[:])
 
-        acc = [ps.tile([P, DV], F32, name=f"acc{h}", tag=f"acc{h}") for h in range(HALVES)]
+        acc = [ps.tile([P, DV], F32, name=f"acc{h}") for h in range(HALVES)]
         for cols in e_halves:
             for h in range(HALVES):
                 nc.tensor.matmul_mx(

@@ -35,21 +35,22 @@ def tile_attend_rel2_cap_topkq256n512t1024_kernel(tc, qT, k_words, k_scales, vT,
         sb = ctx.enter_context(tc.tile_pool(name="sb", bufs=1))
         ps = ctx.enter_context(tc.psum_pool(name="ps", bufs=1))
 
+        def tile(name, shape, dtype, tag=None):
+            return sb.tile(shape, dtype, name=name, tag=tag or name, align_bytes=64)
+
         offsets = sb.tile([P, N // 16], U16, name="offsets")
-        kw_pool = sb.tile([P, T], I32, name="kw_pool", tag="kw_pool", align_bytes=64)
-        kw_rows = k_words[0].rearrange("p t b -> p (t b)").bitcast(I32)
-        q_raw = [sb.tile([P, PACK, NQ], F32, name=f"q_raw{o}", tag=f"q_raw{o}", align_bytes=64) for o in range(PASSES)]
+        q_raw = [tile(f"q_raw{o}", [P, PACK, NQ], F32) for o in range(PASSES)]
         q_rows = qT[0].rearrange("(o p t) q -> o p t q", p=P, t=PACK)
         nc.sync.dma_start(q_raw[0][:], q_rows[0])
         nc.sync.dma_start(offsets[:], offs)
 
-        ks_pool = sb.tile([P, T // 4], I32, name="ks_pool", tag="late", align_bytes=64)
+        ks_pool = tile("ks_pool", [P, T // 4], I32, tag="late")
         nc.vector.memset(ks_pool[:], 0)
         ks_rows = k_scales.bitcast(I32).rearrange("o (g f) t -> f g o t", f=4)
         for f in range(4):
             nc.sync.dma_start(ks_pool[f:P:16, :], ks_rows[f])
-
-        nc.sync.dma_start(kw_pool[:], kw_rows)
+        kw_pool = tile("kw_pool", [P, T], I32)
+        nc.sync.dma_start(kw_pool[:], k_words[0].rearrange("p t b -> p (t b)").bitcast(I32))
         nc.sync.dma_start(q_raw[1][:], q_rows[1])
 
         table_in = sb.tile([P, 1], F32, name="table_in")
@@ -57,182 +58,164 @@ def tile_attend_rel2_cap_topkq256n512t1024_kernel(tc, qT, k_words, k_scales, vT,
         nc.gpsimd.memset(table_in[:], 0.0)
         nc.scalar.activation(table_out[:], table_in[:], ACT.Tanh)
 
-        vs_pool = sb.tile([P, T], F32, name="vs_pool", tag="vs_pool", align_bytes=64)
+        vs_pool = tile("vs_pool", [P, T], F32)
         nc.vector.memset(vs_pool[:], 0.0)
         nc.sync.dma_start(vs_pool[0:1, :], vs[0:1, :])
-        ks_second = sb.tile([P, N // 4], I32, name="ks_second", tag="ks_second", align_bytes=64)
+        ks_second = tile("ks_second", [P, N // 4], I32)
         nc.vector.memset(ks_second[:], 0)
-        ident = sb.tile([P, P], F32, name="ident", align_bytes=64)
+        ident = tile("ident", [P, P], F32)
         make_identity(nc, ident[:])
 
         v_rows = vT.rearrange("(f u) t -> f u t", u=2)
         v_cuts = [0, T // 2, 3 * T // 4, T]
         v_raw = []
-        for c, tag in enumerate(("half0", "half1")):
-            piece = sb.tile([P, 2, v_cuts[c + 1] - v_cuts[c]], F32, name=f"v_raw{c}", tag=tag, align_bytes=64)
-            nc.sync.dma_start(piece[:], v_rows[:, :, v_cuts[c] : v_cuts[c + 1]])
-            v_raw.append(piece)
 
-        def lay_by_place(plane, listed):
-            nc.vector.tensor_copy(
-                plane[:].rearrange("p (t b w) -> p t b w", t=PACK, w=RUN // 4),
-                listed.rearrange("p (b t w) -> p t b w", t=PACK, w=RUN // 4),
-            )
+        def load_values(c, tag):
+            v_raw.append(tile(f"v_raw{c}", [P, 2, v_cuts[c + 1] - v_cuts[c]], F32, tag=tag))
+            nc.sync.dma_start(v_raw[c][:], v_rows[:, :, v_cuts[c] : v_cuts[c + 1]])
 
-        ks_got = sb.tile([P, N], U8, name="ks_got", align_bytes=64)
+        load_values(0, "v_raw0")
+        load_values(1, "v_raw1")
+
+        ks_got = tile("ks_got", [P, N], U8)
         nc.vector.tensor_copy(ks_got[:], ks_pool[:].bitcast(U8).indirect(offsets[:]))
         for lo, hi in ((0, 64), (64, 96), (96, 112)):
             nc.sync.dma_start(ks_second[lo:hi, :], ks_got[lo + 16 : hi + 16, :].bitcast(I32))
-        v_late = sb.tile([P, 2, T // 4], F32, name="v_late", tag="late", align_bytes=64)
-        nc.sync.dma_start(v_late[:], v_rows[:, :, v_cuts[2] :])
-        v_raw.append(v_late)
-        kw_got = sb.tile([P, N], U32, name="kw_got", align_bytes=64)
+        k_planes = [ks_got[:], ks_second[:].bitcast(U8)]
+        load_values(2, "late")
+        kw_got = tile("kw_got", [P, N], U32)
         nc.vector.tensor_copy(kw_got[:], kw_pool[:].bitcast(U32).indirect(offsets[:]))
-        k_codes = sb.tile([P, PASSES, N], U16, name="k_codes", align_bytes=64)
-        nc.vector.tensor_copy(
-            k_codes[:].rearrange("p o (t b j) -> p o t b j", t=PACK, j=RUN),
-            kw_got[:].bitcast(U16).rearrange("p (b t j o) -> p o t b j", t=PACK, j=RUN, o=PASSES),
-        )
+        k_codes = [tile(f"k_codes{o}", [P, N], U16) for o in range(PASSES)]
+        kw_halves = kw_got[:].bitcast(U16).rearrange("p (i o) -> p o i", o=PASSES)
 
-        q_codes = sb.tile([P, HALVES, PASSES, P], U32, name="q_codes", align_bytes=64)
-        q_scales = sb.tile([P, HALVES, PASSES, P], U8, name="q_scales", align_bytes=64)
-        q_bf = [sb.tile([P, PASSES, P, PACK], BF16, name=f"q_bf{h}", tag=f"q_bf{h}", align_bytes=64) for h in range(HALVES)]
-        for o in range(PASSES):
-            for h in range(HALVES):
-                nc.scalar.activation(
-                    q_bf[h][:, o].rearrange("p (c i) t -> p c t i", i=4),
-                    q_raw[o][:, :, h * P : (h + 1) * P].rearrange("p t (c i) -> p c t i", i=4),
-                    ACT.Copy,
-                )
-        plane0 = sb.tile([P, N // 4], I32, name="plane0", tag="q_raw1", align_bytes=64)
-        lay_by_place(plane0, ks_got[:].bitcast(I32))
-        for h in range(HALVES):
-            nc.vector.quantize_mx(
-                out=q_codes[:, h].rearrange("p o q -> p (o q)").bitcast(FP8X4),
-                scales=q_scales[:, h].rearrange("p o q -> p (o q)"),
-                in_=q_bf[h][:].rearrange("p o q t -> p (o q t)"),
+        both = [(o, h) for o in range(PASSES) for h in range(HALVES)]
+        q_bf = [tile(f"q_bf{o}", [P, NQ, PACK], BF16) for o in range(PASSES)]
+        q_codes = [tile("q_codes0", [P, NQ], U32, tag="kw_pool"), tile("q_codes1", [P, NQ], U32)]
+        q_scales = [tile(f"q_scales{o}", [P, NQ], U8) for o in range(PASSES)]
+        q_halves = [slice(h * P, (h + 1) * P) for h in range(HALVES)]
+        for o, h in both:
+            nc.scalar.activation(
+                q_bf[o][:, q_halves[h], :].rearrange("p (c i) t -> p c t i", i=4),
+                q_raw[o][:, :, h * P : (h + 1) * P].rearrange("p t (c i) -> p c t i", i=4),
+                ACT.Copy,
             )
 
-        plane1 = sb.tile([P, N // 4], I32, name="plane1", tag="q_bf0", align_bytes=64)
-        lay_by_place(plane1, ks_second[:])
-        k_planes = [plane0[:].bitcast(U8), plane1[:].bitcast(U8)]
+        def quantize(codes, scales, values):
+            nc.vector.quantize_mx(out=codes.bitcast(FP8X4), scales=scales, in_=values.rearrange("p c t -> p (c t)"))
 
-        scores = [[ps.tile([P, 2, P], F32, name=f"scores{h}{c}", tag=f"bank{h}{c}") for c in range(2)] for h in range(HALVES)]
-        every = [(h, t, o) for h in range(HALVES) for t in range(PACK) for o in range(PASSES)]
-        opening = [(h, t, o) for h, t, o in every if t % 2 == 0 and o == 0]
-        for h, t, o in opening + [x for x in every if x not in opening]:
-            k_cols = slice(t * P, (t + 1) * P)
+        nc.vector.tensor_copy(k_codes[0][:], kw_halves[:, 0, :])
+        quantize(q_codes[0][:], q_scales[0][:], q_bf[0][:])
+        nc.vector.tensor_copy(k_codes[1][:], kw_halves[:, 1, :])
+        for cols in q_halves:
+            quantize(q_codes[1][:, cols], q_scales[1][:, cols], q_bf[1][:, cols, :])
+        vs_got = tile("vs_got", [P, N], U32, tag="q_raw1")
+        nc.vector.tensor_copy(by_place(vs_got[:]), vs_pool[:].bitcast(U32).indirect(offsets[:]))
+
+        scores = [ps.tile([P, N], F32, name=f"scores{h}", tag=f"scores{h}") for h in range(HALVES)]
+        for h, o in both:
             nc.tensor.matmul_mx(
-                out=scores[h][t // 2][:, t % 2, :],
-                lhsT=k_codes[:, o, k_cols].bitcast(FP4X4),
-                lhsT_scale=k_planes[o][:, k_cols],
-                rhs=q_codes[:, h, o, :].bitcast(FP8X4),
-                rhs_scale=q_scales[:, h, o, :],
+                out=scores[h][:],
+                lhsT=q_codes[o][:, q_halves[h]].bitcast(FP8X4),
+                lhsT_scale=q_scales[o][:, q_halves[h]],
+                rhs=k_codes[o][:].bitcast(FP4X4),
+                rhs_scale=k_planes[o],
                 start=(o == 0),
                 stop=(o == PASSES - 1),
             )
 
-        v_pool = sb.tile([P, T, 2], BF16, name="v_pool", tag="v_pool", align_bytes=64)
+        v_pool = tile("v_pool", [P, T, 2], BF16)
         for c in range(3):
             place = v_pool[:, v_cuts[c] : v_cuts[c + 1], :]
             piece = v_raw[c][:].rearrange("p u t -> p t u")
-            if c == 1:
+            if c == 2:
                 nc.vector.tensor_copy(place, piece)
             else:
                 nc.scalar.activation(place, piece, ACT.Copy)
-        vs_got = sb.tile([P, N], U32, name="vs_got", tag="ks_second", align_bytes=64)
-        nc.vector.tensor_copy(by_place(vs_got[:]), vs_pool[:].bitcast(U32).indirect(offsets[:]))
-        v_got = sb.tile([P, N], U32, name="v_got", align_bytes=64)
+        v_got = tile("v_got", [P, N], U32)
         nc.vector.tensor_copy(
             by_place(v_got[:]),
             v_pool[:].rearrange("p t u -> p (t u)").bitcast(U32).indirect(offsets[:]),
         )
 
-        th = [
-            sb.tile([P, PACK, P], F32, name="th0", tag="late", align_bytes=64),
-            sb.tile([P, PACK, P], F32, name="th1", align_bytes=64),
-        ]
-        for h in range(HALVES):
-            for c in range(2):
-                nc.scalar.activation(th[h][:, 2 * c : 2 * c + 2, :], scores[h][c][:], ACT.Tanh, scale=1.0 / CAP)
+        th_both = tile("th_both", [P, HALVES * N], F32)
+        th = [th_both[:, h * N : (h + 1) * N] for h in range(HALVES)]
+        pq = [tile(f"pq{h}", [P, N], F32) for h in range(HALVES)]
+        sums = [tile(f"sums{h}", [P, 1], F32) for h in range(HALVES)]
+        p_turned = [ps.tile([P, PACK, P], F32, name=f"p_turned{h}") for h in range(HALVES)]
+        w_bf = [tile(f"w_bf{h}", [P, P, PACK], BF16) for h in range(HALVES)]
+        w_codes = [tile(f"w_codes{h}", [P, P], U32) for h in range(HALVES)]
+        w_scales = [tile(f"w_scales{h}", [P, P], U8) for h in range(HALVES)]
 
-        vs_turned = ps.tile([P, PACK, P], F32, name="vs_turned", tag="bank00")
-        v_turned = ps.tile([P, PACK, P], F32, name="v_turned", tag="bank01")
-        for t in range(PACK):
-            nc.tensor.transpose(vs_turned[:, t, :], vs_got[:, t * P : (t + 1) * P].bitcast(F32), ident[:])
-        for t in range(PACK):
-            nc.tensor.transpose(v_turned[:, t, :], v_got[:, t * P : (t + 1) * P].bitcast(F32), ident[:])
-        pq = [sb.tile([P, PACK, P], F32, name=f"pq{h}", align_bytes=64) for h in range(HALVES)]
-        positive = sb.tile([P, PACK, P], F32, name="positive", align_bytes=64)
-        pairs = [slice(0, 2), slice(2, 4)]
-        nc.vector.scalar_tensor_tensor(
-            out=pq[0][:], in0=th[0][:], scalar=0.0, in1=th[0][:], op0=ALU.max, op1=ALU.mult
-        )
-        for pair in pairs:
-            nc.scalar.activation(positive[:, pair, :], th[1][:, pair, :], ACT.Relu)
-        for pair in pairs:
-            nc.scalar.activation(pq[1][:, pair, :], positive[:, pair, :], ACT.Square)
-        v_bf = sb.tile([P, DV, PACK], BF16, name="v_bf", align_bytes=64)
-        v_pairs = v_turned[:].bitcast(BF16).rearrange("p t e -> p e t")
-        e_halves = [slice(0, P), slice(P, DV)]
-        for cols in e_halves:
-            nc.scalar.copy(v_bf[:, cols, :], v_pairs[:, cols, :])
-        sums = sb.tile([P, HALVES], F32, name="sums")
-        spill = sb.tile([P, P], BF16, name="spill")
-        for h in range(HALVES):
-            p_turned = ps.tile([P, P], F32, name=f"p_turned{h}")
+        vs_cols = tile("vs_cols", [P, PACK], F32)
+
+        def turn_weights(h):
             for t in range(PACK):
-                nc.tensor.matmul(
-                    p_turned[:], pq[h][:, t, :], ident[:], start=(t == 0), stop=(t == PACK - 1), is_transpose=True
-                )
-            nc.scalar.activation(
-                spill[:], p_turned[:], ACT.Copy, bias=1.0 / (CAP * CAP * P), accum_out=sums[:, h : h + 1]
-            )
+                nc.tensor.transpose(p_turned[h][:, t, :], pq[h][:, t * P : (t + 1) * P], ident[:])
 
-        v_codes = sb.tile([P, DV], U32, name="v_codes", align_bytes=64)
-        v_scales = sb.tile([P, DV], U8, name="v_scales", align_bytes=64)
-        w_bf = [sb.tile([P, P, PACK], BF16, name=f"w_bf{h}", align_bytes=64) for h in range(HALVES)]
-        w_codes = [sb.tile([P, P], U32, name=f"w_codes{h}", align_bytes=64) for h in range(HALVES)]
-        w_scales = [sb.tile([P, P], U8, name=f"w_scales{h}", align_bytes=64) for h in range(HALVES)]
-        vs_cols = vs_turned[:, :, 0:1].unsqueeze(1).broadcast_to([P, P // 4, PACK, 4])
-        for h in range(HALVES):
+        def scale_weights(h):
             nc.vector.tensor_tensor(
-                out=w_bf[h][:].rearrange("p (c i) t -> p c t i", i=4),
-                in0=pq[h][:].rearrange("p t (c i) -> p c t i", i=4),
-                in1=vs_cols,
+                out=w_bf[h][:],
+                in0=p_turned[h][:].rearrange("p t q -> p q t"),
+                in1=vs_cols[:].unsqueeze(1).broadcast_to([P, P, PACK]),
                 op=ALU.mult,
             )
-        for h in range(HALVES):
-            nc.vector.quantize_mx(
-                out=w_codes[h][:].bitcast(FP8X4),
-                scales=w_scales[h][:],
-                in_=w_bf[h][:].rearrange("p q t -> p (q t)"),
-            )
-            nc.vector.quantize_mx(
-                out=v_codes[:, e_halves[h]].bitcast(FP8X4),
-                scales=v_scales[:, e_halves[h]],
-                in_=v_bf[:, e_halves[h], :].rearrange("p e t -> p (e t)"),
-            )
-        inverse = sb.tile([P, HALVES], F32, name="inverse")
-        nc.vector.reciprocal(inverse[:], sums[:])
 
-        acc = [ps.tile([P, DV], F32, name=f"acc{h}") for h in range(HALVES)]
-        for cols in e_halves:
-            for h in range(HALVES):
+        for h in range(HALVES):
+            nc.scalar.activation(
+                th[h].rearrange("p (t b j) -> p t b j", t=PACK, j=RUN),
+                scores[h][:].rearrange("p (b t j) -> p t b j", t=PACK, j=RUN),
+                ACT.Tanh,
+                scale=1.0 / CAP,
+            )
+        vs_turned = ps.tile([P, PACK, P], F32, name="vs_turned", tag="scores0")
+        for t in range(PACK):
+            nc.tensor.transpose(vs_turned[:, t, :], vs_got[:, t * P : (t + 1) * P].bitcast(F32), ident[:])
+        v_turned = ps.tile([P, PACK, P], F32, name="v_turned", tag="scores1")
+        for t in range(PACK):
+            nc.tensor.transpose(v_turned[:, t, :], v_got[:, t * P : (t + 1) * P].bitcast(F32), ident[:])
+        nc.scalar.copy(vs_cols[:], vs_turned[:, :, 0])
+        for h in range(HALVES):
+            nc.vector.scalar_tensor_tensor(
+                out=pq[h][:], in0=th[h], scalar=0.0, in1=th[h], op0=ALU.max, op1=ALU.mult, accum_out=sums[h][:]
+            )
+            turn_weights(h)
+        e_halves = [slice(0, P), slice(P, DV)]
+        v_bf = tile("v_bf", [P, DV, PACK], BF16)
+        v_pairs = v_turned[:].bitcast(BF16).rearrange("p t e -> p e t")
+        for e, cols in enumerate(e_halves):
+            nc.scalar.copy(v_bf[:, cols, :], v_pairs[:, cols, :])
+        totals = tile("totals", [P, HALVES], F32)
+        for h in range(HALVES):
+            nc.gpsimd.tensor_scalar(totals[:, h : h + 1], sums[h][:], 1.0, 1.0 / (CAP * CAP), ALU.mult, ALU.add)
+        inverse = tile("inverse", [P, HALVES], F32)
+        v_codes = [tile(f"v_codes{e}", [P, P], U32) for e in range(2)]
+        v_scales = [tile(f"v_scales{e}", [P, P], U8) for e in range(2)]
+
+        scale_weights(0)
+        quantize(v_codes[0][:], v_scales[0][:], v_bf[:, e_halves[0], :])
+        scale_weights(1)
+        quantize(w_codes[0][:], w_scales[0][:], w_bf[0][:])
+        nc.vector.reciprocal(inverse[:], totals[:])
+        quantize(v_codes[1][:], v_scales[1][:], v_bf[:, e_halves[1], :])
+        quantize(w_codes[1][:], w_scales[1][:], w_bf[1][:])
+
+        banks = {(0, 0): "scores0", (0, 1): "scores1", (1, 0): "acc10", (1, 1): "acc11"}
+        for h in range(HALVES):
+            for e, cols in enumerate(e_halves):
+                acc = ps.tile([P, P], F32, name=f"acc{h}{e}", tag=banks[h, e])
                 nc.tensor.matmul_mx(
-                    out=acc[h][:, cols],
+                    out=acc[:],
                     lhsT=w_codes[h][:].bitcast(FP8X4),
                     lhsT_scale=w_scales[h][:],
-                    rhs=v_codes[:, cols].bitcast(FP8X4),
-                    rhs_scale=v_scales[:, cols],
+                    rhs=v_codes[e][:].bitcast(FP8X4),
+                    rhs_scale=v_scales[e][:],
                     start=True,
                     stop=True,
                 )
-        for h in range(HALVES):
-            y = sb.tile([P, DV], F32, name=f"y{h}", align_bytes=64)
-            if h == 0:
-                nc.scalar.activation(y[:], acc[h][:], ACT.Copy, scale=inverse[:, h : h + 1])
-                nc.scalar.dma_start(out[0, h * P : (h + 1) * P, :], y[:])
-            else:
-                nc.vector.tensor_scalar(y[:], acc[h][:], inverse[:, h : h + 1], None, ALU.mult)
-                nc.sync.dma_start(out[0, h * P : (h + 1) * P, :], y[:])
+                y = tile(f"y{h}{e}", [P, P], F32)
+                if (h, e) == (1, 1):
+                    nc.vector.tensor_scalar(y[:], acc[:], inverse[:, h : h + 1], None, ALU.mult)
+                else:
+                    nc.scalar.activation(y[:], acc[:], ACT.Copy, scale=inverse[:, h : h + 1])
+                queue = nc.scalar if (h, e) == (1, 0) else nc.sync
+                queue.dma_start(out[0, q_halves[h], cols], y[:])

@@ -39,50 +39,53 @@ def tile_attend_rel2_cap_topkq256n512t1024_kernel(tc, qT, k_words, k_scales, vT,
             return sb.tile(shape, dtype, name=name, tag=tag or name, align_bytes=64)
 
         offsets = sb.tile([P, N // 16], U16, name="offsets")
-        q_raw = [tile(f"q_raw{o}", [P, PACK, NQ], F32) for o in range(PASSES)]
-        q_rows = qT[0].rearrange("(o p t) q -> o p t q", p=P, t=PACK)
-        nc.sync.dma_start(q_raw[0][:], q_rows[0])
-        nc.sync.dma_start(offsets[:], offs)
-
-        ks_pool = tile("ks_pool", [P, T // 4], I32, tag="late")
+        ks_pool = tile("ks_pool", [P, T // 4], I32)
         nc.vector.memset(ks_pool[:], 0)
-        ks_rows = k_scales.bitcast(I32).rearrange("o (g f) t -> f g o t", f=4)
-        for f in range(4):
-            nc.sync.dma_start(ks_pool[f:P:16, :], ks_rows[f])
-        kw_pool = tile("kw_pool", [P, T], I32)
-        nc.sync.dma_start(kw_pool[:], k_words[0].rearrange("p t b -> p (t b)").bitcast(I32))
-        nc.sync.dma_start(q_raw[1][:], q_rows[1])
-
         table_in = sb.tile([P, 1], F32, name="table_in")
         table_out = sb.tile([P, 1], F32, name="table_out")
-        nc.gpsimd.memset(table_in[:], 0.0)
-        nc.scalar.activation(table_out[:], table_in[:], ACT.Tanh)
-
+        nc.vector.memset(table_in[:], 0.0)
         vs_pool = tile("vs_pool", [P, T], F32)
         nc.vector.memset(vs_pool[:], 0.0)
+
+        kw_pool = tile("kw_pool", [P, T], I32)
+        kw_rows = k_words[0].rearrange("p t b -> p (t b)").bitcast(I32)
+        nc.sync.dma_start(kw_pool[:, : T // 2], kw_rows[:, : T // 2])
+        nc.sync.dma_start(offsets[:], offs)
+        ks_rows = k_scales.bitcast(I32).rearrange("o (g f) t -> f g o t", f=4)
+        for f in range(4):
+            queue = nc.sync if f % 2 else nc.scalar
+            queue.dma_start(ks_pool[f:P:16, :], ks_rows[f])
+        nc.sync.dma_start(kw_pool[:, T // 2 :], kw_rows[:, T // 2 :])
+        q_raw = [tile(f"q_raw{o}", [P, PACK, NQ], F32) for o in range(PASSES)]
+        q_rows = qT[0].rearrange("(o p t) q -> o p t q", p=P, t=PACK)
+        for o in range(PASSES):
+            nc.sync.dma_start(q_raw[o][:], q_rows[o])
         nc.sync.dma_start(vs_pool[0:1, :], vs[0:1, :])
+
+        nc.scalar.activation(table_out[:], table_in[:], ACT.Tanh)
         ks_second = tile("ks_second", [P, N // 4], I32)
-        nc.vector.memset(ks_second[:], 0)
+        nc.gpsimd.memset(ks_second[:], 0)
+        shrink = tile("shrink", [P, 1], F32)
+        nc.gpsimd.memset(shrink[:], 1.0 / CAP)
         ident = tile("ident", [P, P], F32)
         make_identity(nc, ident[:])
 
         v_rows = vT.rearrange("(f u) t -> f u t", u=2)
         v_cuts = [0, T // 2, 3 * T // 4, T]
-        v_raw = []
+        v_raw = [tile(f"v_raw{c}", [P, 2, v_cuts[c + 1] - v_cuts[c]], F32) for c in range(3)]
 
-        def load_values(c, tag):
-            v_raw.append(tile(f"v_raw{c}", [P, 2, v_cuts[c + 1] - v_cuts[c]], F32, tag=tag))
+        def load_values(c):
             nc.sync.dma_start(v_raw[c][:], v_rows[:, :, v_cuts[c] : v_cuts[c + 1]])
 
-        load_values(0, "v_raw0")
-        load_values(1, "v_raw1")
+        load_values(0)
 
         ks_got = tile("ks_got", [P, N], U8)
         nc.vector.tensor_copy(ks_got[:], ks_pool[:].bitcast(U8).indirect(offsets[:]))
         for lo, hi in ((0, 64), (64, 96), (96, 112)):
             nc.sync.dma_start(ks_second[lo:hi, :], ks_got[lo + 16 : hi + 16, :].bitcast(I32))
         k_planes = [ks_got[:], ks_second[:].bitcast(U8)]
-        load_values(2, "late")
+        load_values(1)
+        load_values(2)
         kw_got = tile("kw_got", [P, N], U32)
         nc.vector.tensor_copy(kw_got[:], kw_pool[:].bitcast(U32).indirect(offsets[:]))
         k_codes = [tile(f"k_codes{o}", [P, N], U16) for o in range(PASSES)]
@@ -90,7 +93,7 @@ def tile_attend_rel2_cap_topkq256n512t1024_kernel(tc, qT, k_words, k_scales, vT,
 
         both = [(o, h) for o in range(PASSES) for h in range(HALVES)]
         q_bf = [tile(f"q_bf{o}", [P, NQ, PACK], BF16) for o in range(PASSES)]
-        q_codes = [tile("q_codes0", [P, NQ], U32, tag="kw_pool"), tile("q_codes1", [P, NQ], U32)]
+        q_codes = [tile(f"q_codes{o}", [P, NQ], U32) for o in range(PASSES)]
         q_scales = [tile(f"q_scales{o}", [P, NQ], U8) for o in range(PASSES)]
         q_halves = [slice(h * P, (h + 1) * P) for h in range(HALVES)]
         for o, h in both:
@@ -103,50 +106,49 @@ def tile_attend_rel2_cap_topkq256n512t1024_kernel(tc, qT, k_words, k_scales, vT,
         def quantize(codes, scales, values):
             nc.vector.quantize_mx(out=codes.bitcast(FP8X4), scales=scales, in_=values.rearrange("p c t -> p (c t)"))
 
+        def quantize_queries(o, h):
+            quantize(q_codes[o][:, q_halves[h]], q_scales[o][:, q_halves[h]], q_bf[o][:, q_halves[h], :])
+
         nc.vector.tensor_copy(k_codes[0][:], kw_halves[:, 0, :])
-        quantize(q_codes[0][:], q_scales[0][:], q_bf[0][:])
+        quantize_queries(0, 0)
         nc.vector.tensor_copy(k_codes[1][:], kw_halves[:, 1, :])
-        for cols in q_halves:
-            quantize(q_codes[1][:, cols], q_scales[1][:, cols], q_bf[1][:, cols, :])
+        quantize_queries(1, 0)
+        quantize_queries(1, 1)
+        quantize_queries(0, 1)
         vs_got = tile("vs_got", [P, N], U32, tag="q_raw1")
         nc.vector.tensor_copy(by_place(vs_got[:]), vs_pool[:].bitcast(U32).indirect(offsets[:]))
 
         scores = [ps.tile([P, N], F32, name=f"scores{h}", tag=f"scores{h}") for h in range(HALVES)]
-        for h, o in both:
+        for h, step in both:
+            o = step if h == 0 else PASSES - 1 - step
             nc.tensor.matmul_mx(
                 out=scores[h][:],
                 lhsT=q_codes[o][:, q_halves[h]].bitcast(FP8X4),
                 lhsT_scale=q_scales[o][:, q_halves[h]],
                 rhs=k_codes[o][:].bitcast(FP4X4),
                 rhs_scale=k_planes[o],
-                start=(o == 0),
-                stop=(o == PASSES - 1),
+                start=(step == 0),
+                stop=(step == PASSES - 1),
             )
 
         v_pool = tile("v_pool", [P, T, 2], BF16)
         for c in range(3):
             place = v_pool[:, v_cuts[c] : v_cuts[c + 1], :]
             piece = v_raw[c][:].rearrange("p u t -> p t u")
-            if c == 2:
+            if c > 0:
                 nc.vector.tensor_copy(place, piece)
             else:
                 nc.scalar.activation(place, piece, ACT.Copy)
-        v_got = tile("v_got", [P, N], U32)
-        nc.vector.tensor_copy(
-            by_place(v_got[:]),
-            v_pool[:].rearrange("p t u -> p (t u)").bitcast(U32).indirect(offsets[:]),
-        )
 
-        th_both = tile("th_both", [P, HALVES * N], F32)
-        th = [th_both[:, h * N : (h + 1) * N] for h in range(HALVES)]
+        th_tiles = [tile(f"th{h}", [P, N], F32) for h in range(HALVES)]
+        th = [x[:] for x in th_tiles]
         pq = [tile(f"pq{h}", [P, N], F32) for h in range(HALVES)]
-        sums = [tile(f"sums{h}", [P, 1], F32) for h in range(HALVES)]
+        positive = tile("positive", [P, N], F32)
+        sums = tile("sums", [P, 3], F32)
         p_turned = [ps.tile([P, PACK, P], F32, name=f"p_turned{h}") for h in range(HALVES)]
         w_bf = [tile(f"w_bf{h}", [P, P, PACK], BF16) for h in range(HALVES)]
-        w_codes = [tile(f"w_codes{h}", [P, P], U32) for h in range(HALVES)]
+        w_codes = []
         w_scales = [tile(f"w_scales{h}", [P, P], U8) for h in range(HALVES)]
-
-        vs_cols = tile("vs_cols", [P, PACK], F32)
 
         def turn_weights(h):
             for t in range(PACK):
@@ -160,49 +162,69 @@ def tile_attend_rel2_cap_topkq256n512t1024_kernel(tc, qT, k_words, k_scales, vT,
                 op=ALU.mult,
             )
 
-        for h in range(HALVES):
+        def by_pair(ap, order, c):
+            return ap.rearrange(order + " -> p t b j", t=PACK, j=RUN)[:, 2 * c : 2 * c + 2]
+
+        nc.scalar.activation(
+            th[0].rearrange("p (t b j) -> p t b j", t=PACK, j=RUN),
+            scores[0][:].rearrange("p (b t j) -> p t b j", t=PACK, j=RUN),
+            ACT.Tanh,
+            scale=shrink[:],
+        )
+        for c in range(2):
             nc.scalar.activation(
-                th[h].rearrange("p (t b j) -> p t b j", t=PACK, j=RUN),
-                scores[h][:].rearrange("p (b t j) -> p t b j", t=PACK, j=RUN),
-                ACT.Tanh,
-                scale=1.0 / CAP,
+                by_pair(th[1], "p (t b j)", c), by_pair(scores[1][:], "p (b t j)", c), ACT.Tanh, scale=1.0 / CAP
             )
         vs_turned = ps.tile([P, PACK, P], F32, name="vs_turned", tag="scores0")
         for t in range(PACK):
             nc.tensor.transpose(vs_turned[:, t, :], vs_got[:, t * P : (t + 1) * P].bitcast(F32), ident[:])
-        v_turned = ps.tile([P, PACK, P], F32, name="v_turned", tag="scores1")
+        nc.vector.scalar_tensor_tensor(
+            out=pq[0][:], in0=th[0], scalar=0.0, in1=th[0], op0=ALU.max, op1=ALU.mult, accum_out=sums[:, 0:1]
+        )
+        turn_weights(0)
+        v_got = tile("v_got", [P, N], U32, tag="shrink")
+        nc.vector.tensor_copy(
+            by_place(v_got[:]),
+            v_pool[:].rearrange("p t u -> p (t u)").bitcast(U32).indirect(offsets[:]),
+        )
+        pair_cols = [slice(c * N // 2, (c + 1) * N // 2) for c in range(2)]
+        for cols in pair_cols:
+            nc.scalar.activation(positive[:, cols], th[1][:, cols], ACT.Relu)
+        for c, cols in enumerate(pair_cols):
+            nc.scalar.activation(pq[1][:, cols], positive[:, cols], ACT.Square, accum_out=sums[:, 1 + c : 2 + c])
+        turn_weights(1)
+        vs_cols = tile("vs_cols", [P, PACK], F32, tag="positive")
+        nc.scalar.copy(vs_cols[:], vs_turned[:, :, 0])
+        v_turned = ps.tile([P, PACK, P], F32, name="v_turned", tag="scores0")
         for t in range(PACK):
             nc.tensor.transpose(v_turned[:, t, :], v_got[:, t * P : (t + 1) * P].bitcast(F32), ident[:])
-        nc.scalar.copy(vs_cols[:], vs_turned[:, :, 0])
-        for h in range(HALVES):
-            nc.vector.scalar_tensor_tensor(
-                out=pq[h][:], in0=th[h], scalar=0.0, in1=th[h], op0=ALU.max, op1=ALU.mult, accum_out=sums[h][:]
-            )
-            turn_weights(h)
+        totals = tile("totals", [P, HALVES], F32)
+        part_total = tile("part_total", [P, 1], F32)
+        nc.scalar.activation(totals[:, 0:1], sums[:, 0:1], ACT.Copy, bias=1.0 / (CAP * CAP))
+        nc.scalar.activation(part_total[:], sums[:, 1:2], ACT.Copy, bias=1.0 / (CAP * CAP))
+        nc.scalar.activation(totals[:, 1:2], sums[:, 2:3], ACT.Identity, bias=part_total[:])
         e_halves = [slice(0, P), slice(P, DV)]
         v_bf = tile("v_bf", [P, DV, PACK], BF16)
         v_pairs = v_turned[:].bitcast(BF16).rearrange("p t e -> p e t")
         for e, cols in enumerate(e_halves):
             nc.scalar.copy(v_bf[:, cols, :], v_pairs[:, cols, :])
-        totals = tile("totals", [P, HALVES], F32)
-        for h in range(HALVES):
-            nc.gpsimd.tensor_scalar(totals[:, h : h + 1], sums[h][:], 1.0, 1.0 / (CAP * CAP), ALU.mult, ALU.add)
-        inverse = tile("inverse", [P, HALVES], F32)
         v_codes = [tile(f"v_codes{e}", [P, P], U32) for e in range(2)]
         v_scales = [tile(f"v_scales{e}", [P, P], U8) for e in range(2)]
 
         scale_weights(0)
-        quantize(v_codes[0][:], v_scales[0][:], v_bf[:, e_halves[0], :])
         scale_weights(1)
+        w_codes.append(tile("w_codes0", [P, P], U32, tag="pq1"))
+        w_codes.append(tile("w_codes1", [P, P], U32))
         quantize(w_codes[0][:], w_scales[0][:], w_bf[0][:])
+        quantize(w_codes[1][:], w_scales[1][:], w_bf[1][:])
+        quantize(v_codes[0][:], v_scales[0][:], v_bf[:, e_halves[0], :])
+        inverse = tile("inverse", [P, HALVES], F32, tag="w_bf0")
         nc.vector.reciprocal(inverse[:], totals[:])
         quantize(v_codes[1][:], v_scales[1][:], v_bf[:, e_halves[1], :])
-        quantize(w_codes[1][:], w_scales[1][:], w_bf[1][:])
 
-        banks = {(0, 0): "scores0", (0, 1): "scores1", (1, 0): "acc10", (1, 1): "acc11"}
-        for h in range(HALVES):
-            for e, cols in enumerate(e_halves):
-                acc = ps.tile([P, P], F32, name=f"acc{h}{e}", tag=banks[h, e])
+        for e, cols in enumerate(e_halves):
+            for h in range(HALVES):
+                acc = ps.tile([P, P], F32, name=f"acc{h}{e}")
                 nc.tensor.matmul_mx(
                     out=acc[:],
                     lhsT=w_codes[h][:].bitcast(FP8X4),
@@ -217,5 +239,5 @@ def tile_attend_rel2_cap_topkq256n512t1024_kernel(tc, qT, k_words, k_scales, vT,
                     nc.vector.tensor_scalar(y[:], acc[:], inverse[:, h : h + 1], None, ALU.mult)
                 else:
                     nc.scalar.activation(y[:], acc[:], ACT.Copy, scale=inverse[:, h : h + 1])
-                queue = nc.scalar if (h, e) == (1, 0) else nc.sync
+                queue = nc.scalar if (h, e) == (0, 1) else nc.sync
                 queue.dma_start(out[0, q_halves[h], cols], y[:])

@@ -39,53 +39,52 @@ def tile_attend_rel2_cap_topkq256n512t1024_kernel(tc, qT, k_words, k_scales, vT,
             return sb.tile(shape, dtype, name=name, tag=tag or name, align_bytes=64)
 
         offsets = sb.tile([P, N // 16], U16, name="offsets")
-        ks_pool = tile("ks_pool", [P, T // 4], I32)
-        nc.vector.memset(ks_pool[:], 0)
-        table_in = sb.tile([P, 1], F32, name="table_in")
-        table_out = sb.tile([P, 1], F32, name="table_out")
-        nc.vector.memset(table_in[:], 0.0)
-        vs_pool = tile("vs_pool", [P, T], F32)
-        nc.vector.memset(vs_pool[:], 0.0)
-
-        kw_pool = tile("kw_pool", [P, T], I32)
-        kw_rows = k_words[0].rearrange("p t b -> p (t b)").bitcast(I32)
-        nc.sync.dma_start(kw_pool[:, : T // 2], kw_rows[:, : T // 2])
-        nc.sync.dma_start(offsets[:], offs)
-        ks_rows = k_scales.bitcast(I32).rearrange("o (g f) t -> f g o t", f=4)
-        for f in range(4):
-            queue = nc.sync if f % 2 else nc.scalar
-            queue.dma_start(ks_pool[f:P:16, :], ks_rows[f])
-        nc.sync.dma_start(kw_pool[:, T // 2 :], kw_rows[:, T // 2 :])
         q_raw = [tile(f"q_raw{o}", [P, PACK, NQ], F32) for o in range(PASSES)]
         q_rows = qT[0].rearrange("(o p t) q -> o p t q", p=P, t=PACK)
-        for o in range(PASSES):
-            nc.sync.dma_start(q_raw[o][:], q_rows[o])
-        nc.sync.dma_start(vs_pool[0:1, :], vs[0:1, :])
+        nc.sync.dma_start(q_raw[0][:], q_rows[0])
+        nc.sync.dma_start(offsets[:], offs)
 
+        ks_pool = tile("ks_pool", [P, T // 4], I32, tag="late")
+        nc.vector.memset(ks_pool[:], 0)
+        ks_rows = k_scales.bitcast(I32).rearrange("o (g f) t -> f g o t", f=4)
+        for f in range(4):
+            nc.sync.dma_start(ks_pool[f:P:16, :], ks_rows[f])
+        kw_pool = tile("kw_pool", [P, T], I32)
+        nc.sync.dma_start(kw_pool[:], k_words[0].rearrange("p t b -> p (t b)").bitcast(I32))
+        nc.sync.dma_start(q_raw[1][:], q_rows[1])
+
+        table_in = sb.tile([P, 1], F32, name="table_in")
+        table_out = sb.tile([P, 1], F32, name="table_out")
+        nc.gpsimd.memset(table_in[:], 0.0)
         nc.scalar.activation(table_out[:], table_in[:], ACT.Tanh)
+
+        vs_pool = tile("vs_pool", [P, T], F32)
+        nc.vector.memset(vs_pool[:], 0.0)
+        nc.sync.dma_start(vs_pool[0:1, :], vs[0:1, :])
         ks_second = tile("ks_second", [P, N // 4], I32)
-        nc.gpsimd.memset(ks_second[:], 0)
-        shrink = tile("shrink", [P, 1], F32)
-        nc.gpsimd.memset(shrink[:], 1.0 / CAP)
+        nc.vector.memset(ks_second[:], 0)
+        minus_one = tile("minus_one", [P, HALVES], F32)
+        nc.gpsimd.memset(minus_one[:], -1.0)
         ident = tile("ident", [P, P], F32)
         make_identity(nc, ident[:])
 
         v_rows = vT.rearrange("(f u) t -> f u t", u=2)
         v_cuts = [0, T // 2, 3 * T // 4, T]
-        v_raw = [tile(f"v_raw{c}", [P, 2, v_cuts[c + 1] - v_cuts[c]], F32) for c in range(3)]
+        v_raw = []
 
-        def load_values(c):
+        def load_values(c, tag):
+            v_raw.append(tile(f"v_raw{c}", [P, 2, v_cuts[c + 1] - v_cuts[c]], F32, tag=tag))
             nc.sync.dma_start(v_raw[c][:], v_rows[:, :, v_cuts[c] : v_cuts[c + 1]])
 
-        load_values(0)
+        load_values(0, "v_raw0")
+        load_values(1, "v_raw1")
 
         ks_got = tile("ks_got", [P, N], U8)
         nc.vector.tensor_copy(ks_got[:], ks_pool[:].bitcast(U8).indirect(offsets[:]))
         for lo, hi in ((0, 64), (64, 96), (96, 112)):
             nc.sync.dma_start(ks_second[lo:hi, :], ks_got[lo + 16 : hi + 16, :].bitcast(I32))
         k_planes = [ks_got[:], ks_second[:].bitcast(U8)]
-        load_values(1)
-        load_values(2)
+        load_values(2, "late")
         kw_got = tile("kw_got", [P, N], U32)
         nc.vector.tensor_copy(kw_got[:], kw_pool[:].bitcast(U32).indirect(offsets[:]))
         k_codes = [tile(f"k_codes{o}", [P, N], U16) for o in range(PASSES)]
@@ -93,7 +92,7 @@ def tile_attend_rel2_cap_topkq256n512t1024_kernel(tc, qT, k_words, k_scales, vT,
 
         both = [(o, h) for o in range(PASSES) for h in range(HALVES)]
         q_bf = [tile(f"q_bf{o}", [P, NQ, PACK], BF16) for o in range(PASSES)]
-        q_codes = [tile(f"q_codes{o}", [P, NQ], U32) for o in range(PASSES)]
+        q_codes = [tile("q_codes0", [P, NQ], U32, tag="kw_pool"), tile("q_codes1", [P, NQ], U32)]
         q_scales = [tile(f"q_scales{o}", [P, NQ], U8) for o in range(PASSES)]
         q_halves = [slice(h * P, (h + 1) * P) for h in range(HALVES)]
         for o, h in both:
@@ -106,15 +105,11 @@ def tile_attend_rel2_cap_topkq256n512t1024_kernel(tc, qT, k_words, k_scales, vT,
         def quantize(codes, scales, values):
             nc.vector.quantize_mx(out=codes.bitcast(FP8X4), scales=scales, in_=values.rearrange("p c t -> p (c t)"))
 
-        def quantize_queries(o, h):
-            quantize(q_codes[o][:, q_halves[h]], q_scales[o][:, q_halves[h]], q_bf[o][:, q_halves[h], :])
-
         nc.vector.tensor_copy(k_codes[0][:], kw_halves[:, 0, :])
-        quantize_queries(0, 0)
+        quantize(q_codes[0][:], q_scales[0][:], q_bf[0][:])
         nc.vector.tensor_copy(k_codes[1][:], kw_halves[:, 1, :])
-        quantize_queries(1, 0)
-        quantize_queries(1, 1)
-        quantize_queries(0, 1)
+        for cols in q_halves:
+            quantize(q_codes[1][:, cols], q_scales[1][:, cols], q_bf[1][:, cols, :])
         vs_got = tile("vs_got", [P, N], U32, tag="q_raw1")
         nc.vector.tensor_copy(by_place(vs_got[:]), vs_pool[:].bitcast(U32).indirect(offsets[:]))
 
@@ -135,92 +130,84 @@ def tile_attend_rel2_cap_topkq256n512t1024_kernel(tc, qT, k_words, k_scales, vT,
         for c in range(3):
             place = v_pool[:, v_cuts[c] : v_cuts[c + 1], :]
             piece = v_raw[c][:].rearrange("p u t -> p t u")
-            if c > 0:
+            if c == 2:
                 nc.vector.tensor_copy(place, piece)
             else:
                 nc.scalar.activation(place, piece, ACT.Copy)
 
-        th_tiles = [tile(f"th{h}", [P, N], F32) for h in range(HALVES)]
-        th = [x[:] for x in th_tiles]
-        pq = [tile(f"pq{h}", [P, N], F32) for h in range(HALVES)]
+        v_got = tile("v_got", [P, N], U32)
+        nc.vector.tensor_copy(
+            by_place(v_got[:]),
+            v_pool[:].rearrange("p t u -> p (t u)").bitcast(U32).indirect(offsets[:]),
+        )
+
+        th = [tile(f"th{h}", [P, N], F32) for h in range(HALVES)]
         positive = tile("positive", [P, N], F32)
+        pq = [tile(f"pq{h}", [P, N], F32) for h in range(HALVES)]
         sums = tile("sums", [P, 3], F32)
         p_turned = [ps.tile([P, PACK, P], F32, name=f"p_turned{h}") for h in range(HALVES)]
         w_bf = [tile(f"w_bf{h}", [P, P, PACK], BF16) for h in range(HALVES)]
-        w_codes = []
         w_scales = [tile(f"w_scales{h}", [P, P], U8) for h in range(HALVES)]
+        pair_cols = [slice(c * N // 2, (c + 1) * N // 2) for c in range(2)]
 
-        def turn_weights(h):
+        def by_pair(ap, order, c):
+            return ap.rearrange(order + " -> p t b j", t=PACK, j=RUN)[:, 2 * c : 2 * c + 2]
+
+        def turn(bank, source):
             for t in range(PACK):
-                nc.tensor.transpose(p_turned[h][:, t, :], pq[h][:, t * P : (t + 1) * P], ident[:])
+                nc.tensor.transpose(bank[:, t, :], source[:, t * P : (t + 1) * P], ident[:])
 
-        def scale_weights(h):
+        for c in range(2):
+            nc.scalar.activation(
+                by_pair(th[0][:], "p (t b j)", c), by_pair(scores[0][:], "p (b t j)", c), ACT.Tanh, scale=1.0 / CAP
+            )
+        nc.scalar.activation(
+            th[1][:].rearrange("p (t b j) -> p t b j", t=PACK, j=RUN),
+            scores[1][:].rearrange("p (b t j) -> p t b j", t=PACK, j=RUN),
+            ACT.Tanh,
+            scale=1.0 / CAP,
+        )
+        vs_turned = ps.tile([P, PACK, P], F32, name="vs_turned", tag="scores0")
+        turn(vs_turned, vs_got[:].bitcast(F32))
+        vs_cols = tile("vs_cols", [P, PACK], F32)
+        nc.scalar.copy(vs_cols[:], vs_turned[:, :, 0])
+        for c, cols in enumerate(pair_cols):
+            nc.gpsimd.tensor_scalar(positive[:, cols], th[0][:, cols], 1.0, 0.0, ALU.min, ALU.max)
+            nc.scalar.activation(pq[0][:, cols], positive[:, cols], ACT.Square, accum_out=sums[:, c : c + 1])
+        turn(p_turned[0], pq[0][:])
+        v_turned = ps.tile([P, PACK, P], F32, name="v_turned", tag="scores1")
+        turn(v_turned, v_got[:].bitcast(F32))
+        nc.vector.scalar_tensor_tensor(
+            out=pq[1][:], in0=th[1][:], scalar=0.0, in1=th[1][:], op0=ALU.max, op1=ALU.mult, accum_out=sums[:, 2:3]
+        )
+        turn(p_turned[1], pq[1][:])
+
+        totals = tile("totals", [P, HALVES], F32)
+        inverse = tile("inverse", [P, HALVES], F32)
+        nc.gpsimd.tensor_scalar(totals[:, 0:1], sums[:, 0:1], sums[:, 1:2], 1.0 / (CAP * CAP), ALU.add, ALU.add)
+        nc.gpsimd.tensor_scalar(totals[:, 1:2], sums[:, 2:3], 1.0, 1.0 / (CAP * CAP), ALU.mult, ALU.add)
+        nc.gpsimd.tensor_tensor(inverse[:], totals[:], minus_one[:], ALU.pow)
+
+        e_halves = [slice(0, P), slice(P, DV)]
+        v_bf = tile("v_bf", [P, DV, PACK], BF16, tag="positive")
+        v_pairs = v_turned[:].bitcast(BF16).rearrange("p t e -> p e t")
+        for cols in e_halves:
+            nc.scalar.copy(v_bf[:, cols, :], v_pairs[:, cols, :])
+        v_codes = [tile(f"v_codes{e}", [P, P], U32) for e in range(2)]
+        v_scales = [tile(f"v_scales{e}", [P, P], U8) for e in range(2)]
+
+        for h in range(HALVES):
             nc.vector.tensor_tensor(
                 out=w_bf[h][:],
                 in0=p_turned[h][:].rearrange("p t q -> p q t"),
                 in1=vs_cols[:].unsqueeze(1).broadcast_to([P, P, PACK]),
                 op=ALU.mult,
             )
-
-        def by_pair(ap, order, c):
-            return ap.rearrange(order + " -> p t b j", t=PACK, j=RUN)[:, 2 * c : 2 * c + 2]
-
-        nc.scalar.activation(
-            th[0].rearrange("p (t b j) -> p t b j", t=PACK, j=RUN),
-            scores[0][:].rearrange("p (b t j) -> p t b j", t=PACK, j=RUN),
-            ACT.Tanh,
-            scale=shrink[:],
-        )
-        for c in range(2):
-            nc.scalar.activation(
-                by_pair(th[1], "p (t b j)", c), by_pair(scores[1][:], "p (b t j)", c), ACT.Tanh, scale=1.0 / CAP
-            )
-        vs_turned = ps.tile([P, PACK, P], F32, name="vs_turned", tag="scores0")
-        for t in range(PACK):
-            nc.tensor.transpose(vs_turned[:, t, :], vs_got[:, t * P : (t + 1) * P].bitcast(F32), ident[:])
-        nc.vector.scalar_tensor_tensor(
-            out=pq[0][:], in0=th[0], scalar=0.0, in1=th[0], op0=ALU.max, op1=ALU.mult, accum_out=sums[:, 0:1]
-        )
-        turn_weights(0)
-        v_got = tile("v_got", [P, N], U32, tag="shrink")
-        nc.vector.tensor_copy(
-            by_place(v_got[:]),
-            v_pool[:].rearrange("p t u -> p (t u)").bitcast(U32).indirect(offsets[:]),
-        )
-        pair_cols = [slice(c * N // 2, (c + 1) * N // 2) for c in range(2)]
-        for cols in pair_cols:
-            nc.scalar.activation(positive[:, cols], th[1][:, cols], ACT.Relu)
-        for c, cols in enumerate(pair_cols):
-            nc.scalar.activation(pq[1][:, cols], positive[:, cols], ACT.Square, accum_out=sums[:, 1 + c : 2 + c])
-        turn_weights(1)
-        vs_cols = tile("vs_cols", [P, PACK], F32, tag="positive")
-        nc.scalar.copy(vs_cols[:], vs_turned[:, :, 0])
-        v_turned = ps.tile([P, PACK, P], F32, name="v_turned", tag="scores0")
-        for t in range(PACK):
-            nc.tensor.transpose(v_turned[:, t, :], v_got[:, t * P : (t + 1) * P].bitcast(F32), ident[:])
-        totals = tile("totals", [P, HALVES], F32)
-        part_total = tile("part_total", [P, 1], F32)
-        nc.scalar.activation(totals[:, 0:1], sums[:, 0:1], ACT.Copy, bias=1.0 / (CAP * CAP))
-        nc.scalar.activation(part_total[:], sums[:, 1:2], ACT.Copy, bias=1.0 / (CAP * CAP))
-        nc.scalar.activation(totals[:, 1:2], sums[:, 2:3], ACT.Identity, bias=part_total[:])
-        e_halves = [slice(0, P), slice(P, DV)]
-        v_bf = tile("v_bf", [P, DV, PACK], BF16)
-        v_pairs = v_turned[:].bitcast(BF16).rearrange("p t e -> p e t")
-        for e, cols in enumerate(e_halves):
-            nc.scalar.copy(v_bf[:, cols, :], v_pairs[:, cols, :])
-        v_codes = [tile(f"v_codes{e}", [P, P], U32) for e in range(2)]
-        v_scales = [tile(f"v_scales{e}", [P, P], U8) for e in range(2)]
-
-        scale_weights(0)
-        scale_weights(1)
-        w_codes.append(tile("w_codes0", [P, P], U32, tag="pq1"))
-        w_codes.append(tile("w_codes1", [P, P], U32))
-        quantize(w_codes[0][:], w_scales[0][:], w_bf[0][:])
-        quantize(w_codes[1][:], w_scales[1][:], w_bf[1][:])
-        quantize(v_codes[0][:], v_scales[0][:], v_bf[:, e_halves[0], :])
-        inverse = tile("inverse", [P, HALVES], F32, tag="w_bf0")
-        nc.vector.reciprocal(inverse[:], totals[:])
-        quantize(v_codes[1][:], v_scales[1][:], v_bf[:, e_halves[1], :])
+        w_codes = [tile("w_codes0", [P, P], U32, tag="pq1"), tile("w_codes1", [P, P], U32)]
+        for x in range(2):
+            quantize(w_codes[x][:], w_scales[x][:], w_bf[x][:])
+        for x in range(2):
+            quantize(v_codes[x][:], v_scales[x][:], v_bf[:, e_halves[x], :])
 
         for e, cols in enumerate(e_halves):
             for h in range(HALVES):

@@ -45,7 +45,8 @@ def tile_attend_rel2_cap_topkq256n512t1024_kernel(tc, qT, k_words, k_scales, vT,
         nc.sync.dma_start(offsets[:], offs)
 
         ks_pool = tile("ks_pool", [P, T // 4], I32, tag="late")
-        nc.vector.memset(ks_pool[:], 0)
+        nc.gpsimd.memset(ks_pool[:, : T // 8], 0)
+        nc.vector.memset(ks_pool[:, T // 8 :], 0)
         ks_rows = k_scales.bitcast(I32).rearrange("o (g f) t -> f g o t", f=4)
         for f in range(4):
             nc.sync.dma_start(ks_pool[f:P:16, :], ks_rows[f])
@@ -60,7 +61,6 @@ def tile_attend_rel2_cap_topkq256n512t1024_kernel(tc, qT, k_words, k_scales, vT,
 
         vs_pool = tile("vs_pool", [P, T], F32)
         nc.vector.memset(vs_pool[:], 0.0)
-        nc.sync.dma_start(vs_pool[0:1, :], vs[0:1, :])
         ks_second = tile("ks_second", [P, N // 4], I32)
         nc.vector.memset(ks_second[:], 0)
         minus_one = tile("minus_one", [P, HALVES], F32)
@@ -78,6 +78,7 @@ def tile_attend_rel2_cap_topkq256n512t1024_kernel(tc, qT, k_words, k_scales, vT,
 
         load_values(0, "v_raw0")
         load_values(1, "v_raw1")
+        nc.sync.dma_start(vs_pool[0:1, :], vs[0:1, :])
 
         ks_got = tile("ks_got", [P, N], U8)
         nc.vector.tensor_copy(ks_got[:], ks_pool[:].bitcast(U8).indirect(offsets[:]))
@@ -86,9 +87,15 @@ def tile_attend_rel2_cap_topkq256n512t1024_kernel(tc, qT, k_words, k_scales, vT,
         k_planes = [ks_got[:], ks_second[:].bitcast(U8)]
         load_values(2, "late")
         kw_got = tile("kw_got", [P, N], U32)
-        nc.vector.tensor_copy(kw_got[:], kw_pool[:].bitcast(U32).indirect(offsets[:]))
-        k_codes = [tile(f"k_codes{o}", [P, N], U16) for o in range(PASSES)]
-        kw_halves = kw_got[:].bitcast(U16).rearrange("p (i o) -> p o i", o=PASSES)
+        slot_halves = [slice(c * N // 2, (c + 1) * N // 2) for c in range(2)]
+        for c, cols in enumerate(slot_halves):
+            listed = offsets[:, c * N // 32 : (c + 1) * N // 32]
+            nc.vector.tensor_copy(kw_got[:, cols], kw_pool[:].bitcast(U32).indirect(listed))
+        k_codes = tile("k_codes", [P, PASSES, N], U16)
+        for cols in slot_halves:
+            nc.vector.tensor_copy(
+                k_codes[:, :, cols], kw_got[:, cols].bitcast(U16).rearrange("p (i o) -> p o i", o=PASSES)
+            )
 
         both = [(o, h) for o in range(PASSES) for h in range(HALVES)]
         q_bf = [tile(f"q_bf{o}", [P, NQ, PACK], BF16) for o in range(PASSES)]
@@ -105,13 +112,9 @@ def tile_attend_rel2_cap_topkq256n512t1024_kernel(tc, qT, k_words, k_scales, vT,
         def quantize(codes, scales, values):
             nc.vector.quantize_mx(out=codes.bitcast(FP8X4), scales=scales, in_=values.rearrange("p c t -> p (c t)"))
 
-        nc.vector.tensor_copy(k_codes[0][:], kw_halves[:, 0, :])
         quantize(q_codes[0][:], q_scales[0][:], q_bf[0][:])
-        nc.vector.tensor_copy(k_codes[1][:], kw_halves[:, 1, :])
         for cols in q_halves:
             quantize(q_codes[1][:, cols], q_scales[1][:, cols], q_bf[1][:, cols, :])
-        vs_got = tile("vs_got", [P, N], U32, tag="q_raw1")
-        nc.vector.tensor_copy(by_place(vs_got[:]), vs_pool[:].bitcast(U32).indirect(offsets[:]))
 
         scores = [ps.tile([P, N], F32, name=f"scores{h}", tag=f"scores{h}") for h in range(HALVES)]
         for h, step in both:
@@ -120,7 +123,7 @@ def tile_attend_rel2_cap_topkq256n512t1024_kernel(tc, qT, k_words, k_scales, vT,
                 out=scores[h][:],
                 lhsT=q_codes[o][:, q_halves[h]].bitcast(FP8X4),
                 lhsT_scale=q_scales[o][:, q_halves[h]],
-                rhs=k_codes[o][:].bitcast(FP4X4),
+                rhs=k_codes[:, o, :].bitcast(FP4X4),
                 rhs_scale=k_planes[o],
                 start=(step == 0),
                 stop=(step == PASSES - 1),
@@ -130,19 +133,22 @@ def tile_attend_rel2_cap_topkq256n512t1024_kernel(tc, qT, k_words, k_scales, vT,
         for c in range(3):
             place = v_pool[:, v_cuts[c] : v_cuts[c + 1], :]
             piece = v_raw[c][:].rearrange("p u t -> p t u")
-            if c == 2:
+            if c == 1:
                 nc.vector.tensor_copy(place, piece)
             else:
                 nc.scalar.activation(place, piece, ACT.Copy)
 
+        vs_got = tile("vs_got", [P, N], U32)
+        nc.vector.tensor_copy(by_place(vs_got[:]), vs_pool[:].bitcast(U32).indirect(offsets[:]))
         v_got = tile("v_got", [P, N], U32)
         nc.vector.tensor_copy(
             by_place(v_got[:]),
             v_pool[:].rearrange("p t u -> p (t u)").bitcast(U32).indirect(offsets[:]),
         )
 
-        th = [tile(f"th{h}", [P, N], F32) for h in range(HALVES)]
-        positive = tile("positive", [P, N], F32)
+        th_both = tile("th_both", [P, HALVES * N], F32, tag="late")
+        th = [th_both[:, h * N : (h + 1) * N] for h in range(HALVES)]
+        positive = tile("positive", [P, N // 2], F32)
         pq = [tile(f"pq{h}", [P, N], F32) for h in range(HALVES)]
         sums = tile("sums", [P, 3], F32)
         p_turned = [ps.tile([P, PACK, P], F32, name=f"p_turned{h}") for h in range(HALVES)]
@@ -159,10 +165,10 @@ def tile_attend_rel2_cap_topkq256n512t1024_kernel(tc, qT, k_words, k_scales, vT,
 
         for c in range(2):
             nc.scalar.activation(
-                by_pair(th[0][:], "p (t b j)", c), by_pair(scores[0][:], "p (b t j)", c), ACT.Tanh, scale=1.0 / CAP
+                by_pair(th[0], "p (t b j)", c), by_pair(scores[0][:], "p (b t j)", c), ACT.Tanh, scale=1.0 / CAP
             )
         nc.scalar.activation(
-            th[1][:].rearrange("p (t b j) -> p t b j", t=PACK, j=RUN),
+            th[1].rearrange("p (t b j) -> p t b j", t=PACK, j=RUN),
             scores[1][:].rearrange("p (b t j) -> p t b j", t=PACK, j=RUN),
             ACT.Tanh,
             scale=1.0 / CAP,
@@ -171,14 +177,23 @@ def tile_attend_rel2_cap_topkq256n512t1024_kernel(tc, qT, k_words, k_scales, vT,
         turn(vs_turned, vs_got[:].bitcast(F32))
         vs_cols = tile("vs_cols", [P, PACK], F32)
         nc.scalar.copy(vs_cols[:], vs_turned[:, :, 0])
-        for c, cols in enumerate(pair_cols):
-            nc.gpsimd.tensor_scalar(positive[:, cols], th[0][:, cols], 1.0, 0.0, ALU.min, ALU.max)
-            nc.scalar.activation(pq[0][:, cols], positive[:, cols], ACT.Square, accum_out=sums[:, c : c + 1])
+        first, second = pair_cols
+        nc.gpsimd.tensor_scalar(positive[:], th[0][:, first], 1.0, 0.0, ALU.min, ALU.max)
+        nc.scalar.activation(pq[0][:, first], positive[:], ACT.Square, accum_out=sums[:, 0:1])
+        nc.vector.scalar_tensor_tensor(
+            out=pq[0][:, second],
+            in0=th[0][:, second],
+            scalar=0.0,
+            in1=th[0][:, second],
+            op0=ALU.max,
+            op1=ALU.mult,
+            accum_out=sums[:, 1:2],
+        )
         turn(p_turned[0], pq[0][:])
         v_turned = ps.tile([P, PACK, P], F32, name="v_turned", tag="scores1")
         turn(v_turned, v_got[:].bitcast(F32))
         nc.vector.scalar_tensor_tensor(
-            out=pq[1][:], in0=th[1][:], scalar=0.0, in1=th[1][:], op0=ALU.max, op1=ALU.mult, accum_out=sums[:, 2:3]
+            out=pq[1][:], in0=th[1], scalar=0.0, in1=th[1], op0=ALU.max, op1=ALU.mult, accum_out=sums[:, 2:3]
         )
         turn(p_turned[1], pq[1][:])
 

@@ -63,8 +63,6 @@ def tile_attend_rel2_cap_topkq256n512t1024_kernel(tc, qT, k_words, k_scales, vT,
         nc.vector.memset(vs_pool[:], 0.0)
         ks_second = tile("ks_second", [P, N // 4], I32)
         nc.vector.memset(ks_second[:], 0)
-        minus_one = tile("minus_one", [P, HALVES], F32)
-        nc.gpsimd.memset(minus_one[:], -1.0)
         ident = tile("ident", [P, P], F32)
         make_identity(nc, ident[:])
 
@@ -198,10 +196,8 @@ def tile_attend_rel2_cap_topkq256n512t1024_kernel(tc, qT, k_words, k_scales, vT,
         turn(p_turned[1], pq[1][:])
 
         totals = tile("totals", [P, HALVES], F32)
-        inverse = tile("inverse", [P, HALVES], F32)
         nc.gpsimd.tensor_scalar(totals[:, 0:1], sums[:, 0:1], sums[:, 1:2], 1.0 / (CAP * CAP), ALU.add, ALU.add)
         nc.gpsimd.tensor_scalar(totals[:, 1:2], sums[:, 2:3], 1.0, 1.0 / (CAP * CAP), ALU.mult, ALU.add)
-        nc.gpsimd.tensor_tensor(inverse[:], totals[:], minus_one[:], ALU.pow)
 
         e_halves = [slice(0, P), slice(P, DV)]
         v_bf = tile("v_bf", [P, DV, PACK], BF16, tag="positive")
@@ -221,6 +217,8 @@ def tile_attend_rel2_cap_topkq256n512t1024_kernel(tc, qT, k_words, k_scales, vT,
         w_codes = [tile("w_codes0", [P, P], U32, tag="pq1"), tile("w_codes1", [P, P], U32)]
         for x in range(2):
             quantize(w_codes[x][:], w_scales[x][:], w_bf[x][:])
+        inverse = tile("inverse", [P, HALVES], F32, tag="w_bf0")
+        nc.vector.reciprocal(inverse[:], totals[:])
         for x in range(2):
             quantize(v_codes[x][:], v_scales[x][:], v_bf[:, e_halves[x], :])
 

@@ -25,8 +25,8 @@ CAP = 2.0
 FLOPS = 2 * NQ * N * (D + DV)
 
 
-def by_place(ap):
-    return ap.rearrange("p (t b j) -> p b t j", t=PACK, j=RUN)
+def by_pair(ap):
+    return ap.rearrange("p (c b x) -> p b c x", c=2, x=2 * RUN)
 
 
 def tile_attend_rel2_cap_topkq256n512t1024_kernel(tc, qT, k_words, k_scales, vT, vs, offs, out):
@@ -41,49 +41,40 @@ def tile_attend_rel2_cap_topkq256n512t1024_kernel(tc, qT, k_words, k_scales, vT,
         offsets = sb.tile([P, N // 16], U16, name="offsets")
         q_raw = [tile(f"q_raw{o}", [P, PACK, NQ], F32) for o in range(PASSES)]
         q_rows = qT[0].rearrange("(o p t) q -> o p t q", p=P, t=PACK)
-        nc.sync.dma_start(q_raw[0][:], q_rows[0])
+        ks_pool = tile("ks_pool", [P, T // 4], I32)
+        nc.sync.dma_start(ks_pool[0:32, :], k_scales.bitcast(I32).rearrange("o r t -> r o t"))
         nc.sync.dma_start(offsets[:], offs)
-
-        ks_pool = tile("ks_pool", [P, T // 4], I32, tag="late")
-        nc.gpsimd.memset(ks_pool[:, : T // 8], 0)
-        nc.vector.memset(ks_pool[:, T // 8 :], 0)
-        ks_rows = k_scales.bitcast(I32).rearrange("o (g f) t -> f g o t", f=4)
-        for f in range(4):
-            nc.sync.dma_start(ks_pool[f:P:16, :], ks_rows[f])
         kw_pool = tile("kw_pool", [P, T], I32)
         nc.sync.dma_start(kw_pool[:], k_words[0].rearrange("p t b -> p (t b)").bitcast(I32))
+        vs_pool = tile("vs_pool", [P, T], F32)
+        nc.vector.memset(vs_pool[:, : T // 2], 0.0)
+        nc.gpsimd.memset(vs_pool[:, T // 2 :], 0.0)
+        nc.sync.dma_start(q_raw[0][:], q_rows[0])
         nc.sync.dma_start(q_raw[1][:], q_rows[1])
+        nc.sync.dma_start(vs_pool[0:1, :], vs[0:1, :])
+        nc.vector.memset(ks_pool[32:64, :], 0)
+        nc.vector.memset(ks_pool[64:128, :], 0)
 
         table_in = sb.tile([P, 1], F32, name="table_in")
         table_out = sb.tile([P, 1], F32, name="table_out")
         nc.gpsimd.memset(table_in[:], 0.0)
         nc.scalar.activation(table_out[:], table_in[:], ACT.Tanh)
 
-        vs_pool = tile("vs_pool", [P, T], F32)
-        nc.vector.memset(vs_pool[:], 0.0)
-        ks_second = tile("ks_second", [P, N // 4], I32)
-        nc.vector.memset(ks_second[:], 0)
+        ks_planes = tile("ks_planes", [P, PASSES * N // 4], I32)
+        nc.vector.memset(ks_planes[:], 0)
         ident = tile("ident", [P, P], F32)
         make_identity(nc, ident[:])
 
-        v_rows = vT.rearrange("(f u) t -> f u t", u=2)
-        v_cuts = [0, T // 2, 3 * T // 4, T]
-        v_raw = []
-
-        def load_values(c, tag):
-            v_raw.append(tile(f"v_raw{c}", [P, 2, v_cuts[c + 1] - v_cuts[c]], F32, tag=tag))
-            nc.sync.dma_start(v_raw[c][:], v_rows[:, :, v_cuts[c] : v_cuts[c + 1]])
-
-        load_values(0, "v_raw0")
-        load_values(1, "v_raw1")
-        nc.sync.dma_start(vs_pool[0:1, :], vs[0:1, :])
+        v_pool = [tile(f"v_pool{e}", [P, T], F32) for e in range(2)]
+        nc.sync.dma_start(v_pool[0][:, : T // 2], vT[:P, : T // 2])
 
         ks_got = tile("ks_got", [P, N], U8)
         nc.vector.tensor_copy(ks_got[:], ks_pool[:].bitcast(U8).indirect(offsets[:]))
-        for lo, hi in ((0, 64), (64, 96), (96, 112)):
-            nc.sync.dma_start(ks_second[lo:hi, :], ks_got[lo + 16 : hi + 16, :].bitcast(I32))
-        k_planes = [ks_got[:], ks_second[:].bitcast(U8)]
-        load_values(2, "late")
+        for g in range(4):
+            nc.sync.dma_start(ks_planes[32 * g : 32 * g + 4, :], ks_got[8 * g : 8 * g + 8, :].bitcast(I32))
+        k_planes = [ks_planes[:].bitcast(U8)[:, o * N : (o + 1) * N] for o in range(PASSES)]
+        nc.sync.dma_start(v_pool[0][:, T // 2 :], vT[:P, T // 2 :])
+        nc.sync.dma_start(v_pool[1][:], vT[P:, :])
         kw_got = tile("kw_got", [P, N], U32)
         slot_halves = [slice(c * N // 2, (c + 1) * N // 2) for c in range(2)]
         for c, cols in enumerate(slot_halves):
@@ -97,8 +88,8 @@ def tile_attend_rel2_cap_topkq256n512t1024_kernel(tc, qT, k_words, k_scales, vT,
 
         both = [(o, h) for o in range(PASSES) for h in range(HALVES)]
         q_bf = [tile(f"q_bf{o}", [P, NQ, PACK], BF16) for o in range(PASSES)]
-        q_codes = [tile("q_codes0", [P, NQ], U32, tag="kw_pool"), tile("q_codes1", [P, NQ], U32)]
-        q_scales = [tile(f"q_scales{o}", [P, NQ], U8) for o in range(PASSES)]
+        q_codes = {(o, h): tile(f"q_codes{o}{h}", [P, P], U32) for o, h in both}
+        q_scales = {(o, h): tile(f"q_scales{o}{h}", [P, P], U8) for o, h in both}
         q_halves = [slice(h * P, (h + 1) * P) for h in range(HALVES)]
         for o, h in both:
             nc.scalar.activation(
@@ -110,100 +101,114 @@ def tile_attend_rel2_cap_topkq256n512t1024_kernel(tc, qT, k_words, k_scales, vT,
         def quantize(codes, scales, values):
             nc.vector.quantize_mx(out=codes.bitcast(FP8X4), scales=scales, in_=values.rearrange("p c t -> p (c t)"))
 
-        quantize(q_codes[0][:], q_scales[0][:], q_bf[0][:])
-        for cols in q_halves:
-            quantize(q_codes[1][:, cols], q_scales[1][:, cols], q_bf[1][:, cols, :])
+        vs_got = tile("vs_got", [P, N], U32)
+        for o, h in both:
+            if (o, h) == both[-1]:
+                nc.vector.tensor_copy(by_pair(vs_got[:]), vs_pool[:].bitcast(U32).indirect(offsets[:]))
+            quantize(q_codes[o, h][:], q_scales[o, h][:], q_bf[o][:, q_halves[h], :])
 
         scores = [ps.tile([P, N], F32, name=f"scores{h}", tag=f"scores{h}") for h in range(HALVES)]
-        for h, step in both:
-            o = step if h == 0 else PASSES - 1 - step
+        for h, o in both:
             nc.tensor.matmul_mx(
                 out=scores[h][:],
-                lhsT=q_codes[o][:, q_halves[h]].bitcast(FP8X4),
-                lhsT_scale=q_scales[o][:, q_halves[h]],
+                lhsT=q_codes[o, h][:].bitcast(FP8X4),
+                lhsT_scale=q_scales[o, h][:],
                 rhs=k_codes[:, o, :].bitcast(FP4X4),
                 rhs_scale=k_planes[o],
-                start=(step == 0),
-                stop=(step == PASSES - 1),
+                start=(o == 0),
+                stop=(o == PASSES - 1),
             )
 
-        v_pool = tile("v_pool", [P, T, 2], BF16)
-        for c in range(3):
-            place = v_pool[:, v_cuts[c] : v_cuts[c + 1], :]
-            piece = v_raw[c][:].rearrange("p u t -> p t u")
-            if c == 1:
-                nc.vector.tensor_copy(place, piece)
-            else:
-                nc.scalar.activation(place, piece, ACT.Copy)
+        v_got = [tile(f"v_got{e}", [P, N], BF16) for e in range(2)]
+        for e in range(2):
+            nc.vector.tensor_copy(by_pair(v_got[e][:]), v_pool[e][:].indirect(offsets[:]))
 
-        vs_got = tile("vs_got", [P, N], U32)
-        nc.vector.tensor_copy(by_place(vs_got[:]), vs_pool[:].bitcast(U32).indirect(offsets[:]))
-        v_got = tile("v_got", [P, N], U32)
-        nc.vector.tensor_copy(
-            by_place(v_got[:]),
-            v_pool[:].rearrange("p t u -> p (t u)").bitcast(U32).indirect(offsets[:]),
-        )
-
-        th_both = tile("th_both", [P, HALVES * N], F32, tag="late")
-        th = [th_both[:, h * N : (h + 1) * N] for h in range(HALVES)]
-        positive = tile("positive", [P, N // 2], F32)
+        th = [tile(f"th{h}", [P, N], F32) for h in range(HALVES)]
+        positive = [tile(f"positive{h}", [P, N], F32) for h in range(HALVES)]
         pq = [tile(f"pq{h}", [P, N], F32) for h in range(HALVES)]
-        sums = tile("sums", [P, 3], F32)
+        sums = tile("sums", [P, 2 * HALVES], F32)
         p_turned = [ps.tile([P, PACK, P], F32, name=f"p_turned{h}") for h in range(HALVES)]
         w_bf = [tile(f"w_bf{h}", [P, P, PACK], BF16) for h in range(HALVES)]
         w_scales = [tile(f"w_scales{h}", [P, P], U8) for h in range(HALVES)]
         pair_cols = [slice(c * N // 2, (c + 1) * N // 2) for c in range(2)]
 
-        def by_pair(ap, order, c):
-            return ap.rearrange(order + " -> p t b j", t=PACK, j=RUN)[:, 2 * c : 2 * c + 2]
-
         def turn(bank, source):
             for t in range(PACK):
                 nc.tensor.transpose(bank[:, t, :], source[:, t * P : (t + 1) * P], ident[:])
 
-        for c in range(2):
+        def cap(h, c):
             nc.scalar.activation(
-                by_pair(th[0], "p (t b j)", c), by_pair(scores[0][:], "p (b t j)", c), ACT.Tanh, scale=1.0 / CAP
+                th[h][:, pair_cols[c]].rearrange("p (e b j) -> p e b j", e=2, j=RUN),
+                scores[h][:].rearrange("p (b c j e) -> p c e b j", c=2, j=RUN, e=2)[:, c],
+                ACT.Tanh,
+                scale=1.0 / CAP,
             )
-        nc.scalar.activation(
-            th[1].rearrange("p (t b j) -> p t b j", t=PACK, j=RUN),
-            scores[1][:].rearrange("p (b t j) -> p t b j", t=PACK, j=RUN),
-            ACT.Tanh,
-            scale=1.0 / CAP,
-        )
+
+        def clamp(h, c):
+            nc.gpsimd.tensor_scalar(positive[h][:, pair_cols[c]], th[h][:, pair_cols[c]], 1.0, 0.0, ALU.min, ALU.max)
+
+        def square(h, c):
+            nc.scalar.activation(
+                pq[h][:, pair_cols[c]],
+                positive[h][:, pair_cols[c]],
+                ACT.Square,
+                accum_out=sums[:, 2 * h + c : 2 * h + c + 1],
+            )
+
+        v_bf = [tile(f"v_bf{e}", [P, P, PACK], BF16) for e in range(2)]
+
+        def turn_values(e, tag):
+            bank = ps.tile([P, 2, P], F32, name=f"v_turned{e}", tag=tag)
+            words = v_got[e][:].bitcast(F32)
+            for c in range(2):
+                nc.tensor.transpose(bank[:, c, :], words[:, c * P : (c + 1) * P], ident[:])
+            nc.scalar.copy(
+                v_bf[e][:].rearrange("p f t -> p (f t)").bitcast(F32).rearrange("p (f c) -> p f c", c=2),
+                bank[:].rearrange("p c f -> p f c"),
+            )
+
+        cap(0, 1)
+        cap(0, 0)
+        clamp(0, 0)
+        nc.scalar.activation(positive[0][:, pair_cols[1]], th[0][:, pair_cols[1]], ACT.Relu)
+        cap(1, 0)
+        clamp(1, 0)
+        square(0, 1)
+        square(0, 0)
         vs_turned = ps.tile([P, PACK, P], F32, name="vs_turned", tag="scores0")
-        turn(vs_turned, vs_got[:].bitcast(F32))
+        for t in range(PACK):
+            first = (t // 2) * N // 2 + t % 2
+            nc.tensor.transpose(vs_turned[:, t, :], vs_got[:].bitcast(F32)[:, first : first + N // 2 - t % 2 : 2], ident[:])
         vs_cols = tile("vs_cols", [P, PACK], F32)
         nc.scalar.copy(vs_cols[:], vs_turned[:, :, 0])
-        first, second = pair_cols
-        nc.gpsimd.tensor_scalar(positive[:], th[0][:, first], 1.0, 0.0, ALU.min, ALU.max)
-        nc.scalar.activation(pq[0][:, first], positive[:], ACT.Square, accum_out=sums[:, 0:1])
+        cap(1, 1)
+        turn(p_turned[0], pq[0][:])
+        square(1, 0)
         nc.vector.scalar_tensor_tensor(
-            out=pq[0][:, second],
-            in0=th[0][:, second],
+            out=pq[1][:, pair_cols[1]],
+            in0=th[1][:, pair_cols[1]],
             scalar=0.0,
-            in1=th[0][:, second],
+            in1=th[1][:, pair_cols[1]],
             op0=ALU.max,
             op1=ALU.mult,
-            accum_out=sums[:, 1:2],
+            accum_out=sums[:, 3:4],
         )
-        turn(p_turned[0], pq[0][:])
-        v_turned = ps.tile([P, PACK, P], F32, name="v_turned", tag="scores1")
-        turn(v_turned, v_got[:].bitcast(F32))
-        nc.vector.scalar_tensor_tensor(
-            out=pq[1][:], in0=th[1], scalar=0.0, in1=th[1], op0=ALU.max, op1=ALU.mult, accum_out=sums[:, 2:3]
-        )
+        turn_values(0, "scores0")
         turn(p_turned[1], pq[1][:])
+        turn_values(1, "scores1")
 
         totals = tile("totals", [P, HALVES], F32)
-        nc.gpsimd.tensor_scalar(totals[:, 0:1], sums[:, 0:1], sums[:, 1:2], 1.0 / (CAP * CAP), ALU.add, ALU.add)
-        nc.gpsimd.tensor_scalar(totals[:, 1:2], sums[:, 2:3], 1.0, 1.0 / (CAP * CAP), ALU.mult, ALU.add)
+        for h in range(HALVES):
+            nc.gpsimd.tensor_scalar(
+                totals[:, h : h + 1],
+                sums[:, 2 * h : 2 * h + 1],
+                sums[:, 2 * h + 1 : 2 * h + 2],
+                1.0 / (CAP * CAP),
+                ALU.add,
+                ALU.add,
+            )
 
         e_halves = [slice(0, P), slice(P, DV)]
-        v_bf = tile("v_bf", [P, DV, PACK], BF16, tag="positive")
-        v_pairs = v_turned[:].bitcast(BF16).rearrange("p t e -> p e t")
-        for cols in e_halves:
-            nc.scalar.copy(v_bf[:, cols, :], v_pairs[:, cols, :])
         v_codes = [tile(f"v_codes{e}", [P, P], U32) for e in range(2)]
         v_scales = [tile(f"v_scales{e}", [P, P], U8) for e in range(2)]
 
@@ -214,13 +219,13 @@ def tile_attend_rel2_cap_topkq256n512t1024_kernel(tc, qT, k_words, k_scales, vT,
                 in1=vs_cols[:].unsqueeze(1).broadcast_to([P, P, PACK]),
                 op=ALU.mult,
             )
-        w_codes = [tile("w_codes0", [P, P], U32, tag="pq1"), tile("w_codes1", [P, P], U32)]
+        w_codes = [tile("w_codes0", [P, P], U32), tile("w_codes1", [P, P], U32)]
         for x in range(2):
             quantize(w_codes[x][:], w_scales[x][:], w_bf[x][:])
         inverse = tile("inverse", [P, HALVES], F32, tag="w_bf0")
         nc.vector.reciprocal(inverse[:], totals[:])
         for x in range(2):
-            quantize(v_codes[x][:], v_scales[x][:], v_bf[:, e_halves[x], :])
+            quantize(v_codes[x][:], v_scales[x][:], v_bf[x][:])
 
         for e, cols in enumerate(e_halves):
             for h in range(HALVES):

@@ -16,17 +16,12 @@ ALU = mybir.AluOpType
 
 P = 128
 PACK = 4
-RUN = 8
 N, T, D, DV, NQ = 512, 1024, 1024, 256, 256
 PASSES = D // (P * PACK)
 HALVES = NQ // P
 CAP = 2.0
 
 FLOPS = 2 * NQ * N * (D + DV)
-
-
-def by_pair(ap):
-    return ap.rearrange("p (c b x) -> p b c x", c=2, x=2 * RUN)
 
 
 def tile_attend_rel2_cap_topkq256n512t1024_kernel(tc, qT, k_words, k_scales, vT, vs, offs, out):
@@ -66,14 +61,13 @@ def tile_attend_rel2_cap_topkq256n512t1024_kernel(tc, qT, k_words, k_scales, vT,
         make_identity(nc, ident[:])
 
         v_pool = [tile(f"v_pool{e}", [P, T], F32) for e in range(2)]
-        nc.sync.dma_start(v_pool[0][:, : T // 2], vT[:P, : T // 2])
 
         ks_got = tile("ks_got", [P, N], U8)
         nc.vector.tensor_copy(ks_got[:], ks_pool[:].bitcast(U8).indirect(offsets[:]))
         for g in range(4):
             nc.sync.dma_start(ks_planes[32 * g : 32 * g + 4, :], ks_got[8 * g : 8 * g + 8, :].bitcast(I32))
         k_planes = [ks_planes[:].bitcast(U8)[:, o * N : (o + 1) * N] for o in range(PASSES)]
-        nc.sync.dma_start(v_pool[0][:, T // 2 :], vT[:P, T // 2 :])
+        nc.sync.dma_start(v_pool[0][:], vT[:P, :])
         nc.sync.dma_start(v_pool[1][:], vT[P:, :])
         kw_got = tile("kw_got", [P, N], U32)
         slot_halves = [slice(c * N // 2, (c + 1) * N // 2) for c in range(2)]
@@ -101,11 +95,14 @@ def tile_attend_rel2_cap_topkq256n512t1024_kernel(tc, qT, k_words, k_scales, vT,
         def quantize(codes, scales, values):
             nc.vector.quantize_mx(out=codes.bitcast(FP8X4), scales=scales, in_=values.rearrange("p c t -> p (c t)"))
 
-        vs_got = tile("vs_got", [P, N], U32)
+        vs_got = tile("vs_got", [P, N], F32)
         for o, h in both:
             if (o, h) == both[-1]:
-                nc.vector.tensor_copy(by_pair(vs_got[:]), vs_pool[:].bitcast(U32).indirect(offsets[:]))
+                nc.vector.tensor_copy(vs_got[:], vs_pool[:].indirect(offsets[:]))
             quantize(q_codes[o, h][:], q_scales[o, h][:], q_bf[o][:, q_halves[h], :])
+
+        vs_cols = tile("vs_cols", [P, PACK], F32)
+        nc.sync.dma_start(vs_cols[:], vs_got[0:1, :])
 
         scores = [ps.tile([P, N], F32, name=f"scores{h}", tag=f"scores{h}") for h in range(HALVES)]
         for h, o in both:
@@ -121,7 +118,7 @@ def tile_attend_rel2_cap_topkq256n512t1024_kernel(tc, qT, k_words, k_scales, vT,
 
         v_got = [tile(f"v_got{e}", [P, N], BF16) for e in range(2)]
         for e in range(2):
-            nc.vector.tensor_copy(by_pair(v_got[e][:]), v_pool[e][:].indirect(offsets[:]))
+            nc.vector.tensor_copy(v_got[e][:], v_pool[e][:].indirect(offsets[:]))
 
         th = [tile(f"th{h}", [P, N], F32) for h in range(HALVES)]
         positive = [tile(f"positive{h}", [P, N], F32) for h in range(HALVES)]
@@ -138,8 +135,8 @@ def tile_attend_rel2_cap_topkq256n512t1024_kernel(tc, qT, k_words, k_scales, vT,
 
         def cap(h, c):
             nc.scalar.activation(
-                th[h][:, pair_cols[c]].rearrange("p (e b j) -> p e b j", e=2, j=RUN),
-                scores[h][:].rearrange("p (b c j e) -> p c e b j", c=2, j=RUN, e=2)[:, c],
+                th[h][:, pair_cols[c]].rearrange("p (t s) -> p t s", t=2),
+                scores[h][:].rearrange("p (s t) -> p t s", t=PACK)[:, 2 * c : 2 * c + 2],
                 ACT.Tanh,
                 scale=1.0 / CAP,
             )
@@ -155,13 +152,13 @@ def tile_attend_rel2_cap_topkq256n512t1024_kernel(tc, qT, k_words, k_scales, vT,
                 accum_out=sums[:, 2 * h + c : 2 * h + c + 1],
             )
 
-        v_bf = [tile(f"v_bf{e}", [P, P, PACK], BF16) for e in range(2)]
+        v_bf = [tile("v_bf0", [P, P, PACK], BF16, tag="positive1"), tile("v_bf1", [P, P, PACK], BF16)]
 
         def turn_values(e, tag):
             bank = ps.tile([P, 2, P], F32, name=f"v_turned{e}", tag=tag)
             words = v_got[e][:].bitcast(F32)
             for c in range(2):
-                nc.tensor.transpose(bank[:, c, :], words[:, c * P : (c + 1) * P], ident[:])
+                nc.tensor.transpose(bank[:, c, :], words[:, c : N // 2 : 2], ident[:])
             nc.scalar.copy(
                 v_bf[e][:].rearrange("p f t -> p (f t)").bitcast(F32).rearrange("p (f c) -> p f c", c=2),
                 bank[:].rearrange("p c f -> p f c"),
@@ -175,12 +172,6 @@ def tile_attend_rel2_cap_topkq256n512t1024_kernel(tc, qT, k_words, k_scales, vT,
         clamp(1, 0)
         square(0, 1)
         square(0, 0)
-        vs_turned = ps.tile([P, PACK, P], F32, name="vs_turned", tag="scores0")
-        for t in range(PACK):
-            first = (t // 2) * N // 2 + t % 2
-            nc.tensor.transpose(vs_turned[:, t, :], vs_got[:].bitcast(F32)[:, first : first + N // 2 - t % 2 : 2], ident[:])
-        vs_cols = tile("vs_cols", [P, PACK], F32)
-        nc.scalar.copy(vs_cols[:], vs_turned[:, :, 0])
         cap(1, 1)
         turn(p_turned[0], pq[0][:])
         square(1, 0)

@@ -65,7 +65,8 @@ def tile_attend_rel2_cap_topkq256n512t1024_kernel(tc, qT, k_words, k_scales, vT,
         ks_got = tile("ks_got", [P, N], U8)
         nc.vector.tensor_copy(ks_got[:], ks_pool[:].bitcast(U8).indirect(offsets[:]))
         for g in range(4):
-            nc.sync.dma_start(ks_planes[32 * g : 32 * g + 4, :], ks_got[8 * g : 8 * g + 8, :].bitcast(I32))
+            queue = nc.sync if g % 2 == 0 else nc.scalar
+            queue.dma_start(ks_planes[32 * g : 32 * g + 4, :], ks_got[8 * g : 8 * g + 8, :].bitcast(I32))
         k_planes = [ks_planes[:].bitcast(U8)[:, o * N : (o + 1) * N] for o in range(PASSES)]
         nc.sync.dma_start(v_pool[0][:], vT[:P, :])
         nc.sync.dma_start(v_pool[1][:], vT[P:, :])
@@ -200,26 +201,24 @@ def tile_attend_rel2_cap_topkq256n512t1024_kernel(tc, qT, k_words, k_scales, vT,
             )
 
         e_halves = [slice(0, P), slice(P, DV)]
-        v_codes = [tile(f"v_codes{e}", [P, P], U32) for e in range(2)]
+        v_codes = [tile(f"v_codes{e}", [P, P], U32, tag=f"pq{e}") for e in range(2)]
         v_scales = [tile(f"v_scales{e}", [P, P], U8) for e in range(2)]
-
-        for h in range(HALVES):
+        w_codes = [tile(f"w_codes{h}", [P, P], U32) for h in range(HALVES)]
+        for x in range(2):
             nc.vector.tensor_tensor(
-                out=w_bf[h][:],
-                in0=p_turned[h][:].rearrange("p t q -> p q t"),
+                out=w_bf[x][:],
+                in0=p_turned[x][:].rearrange("p t q -> p q t"),
                 in1=vs_cols[:].unsqueeze(1).broadcast_to([P, P, PACK]),
                 op=ALU.mult,
             )
-        w_codes = [tile("w_codes0", [P, P], U32), tile("w_codes1", [P, P], U32)]
-        for x in range(2):
-            quantize(w_codes[x][:], w_scales[x][:], w_bf[x][:])
-        inverse = tile("inverse", [P, HALVES], F32, tag="w_bf0")
-        nc.vector.reciprocal(inverse[:], totals[:])
-        for x in range(2):
             quantize(v_codes[x][:], v_scales[x][:], v_bf[x][:])
+            quantize(w_codes[x][:], w_scales[x][:], w_bf[x][:])
+            if x == 0:
+                inverse = tile("inverse", [P, HALVES], F32)
+                nc.vector.reciprocal(inverse[:], totals[:])
 
-        for e, cols in enumerate(e_halves):
-            for h in range(HALVES):
+        for h in range(HALVES):
+            for e, cols in enumerate(e_halves):
                 acc = ps.tile([P, P], F32, name=f"acc{h}{e}")
                 nc.tensor.matmul_mx(
                     out=acc[:],
@@ -231,9 +230,9 @@ def tile_attend_rel2_cap_topkq256n512t1024_kernel(tc, qT, k_words, k_scales, vT,
                     stop=True,
                 )
                 y = tile(f"y{h}{e}", [P, P], F32)
-                if (h, e) == (1, 1):
+                if (h, e) == (1, 0):
                     nc.vector.tensor_scalar(y[:], acc[:], inverse[:, h : h + 1], None, ALU.mult)
                 else:
                     nc.scalar.activation(y[:], acc[:], ACT.Copy, scale=inverse[:, h : h + 1])
-                queue = nc.scalar if (h, e) == (0, 1) else nc.sync
+                queue = nc.scalar if (h, e) == (1, 1) else nc.sync
                 queue.dma_start(out[0, q_halves[h], cols], y[:])

@@ -20,6 +20,8 @@ N, T, D, DV, NQ = 512, 1024, 1024, 256, 256
 PASSES = D // (P * PACK)
 HALVES = NQ // P
 CAP = 2.0
+OVERLAP = 64
+VS_FIRST = 128
 
 FLOPS = 2 * NQ * N * (D + DV)
 
@@ -34,7 +36,12 @@ def tile_attend_rel2_cap_topkq256n512t1024_kernel(tc, qT, k_words, k_scales, vT,
             return sb.tile(shape, dtype, name=name, tag=tag or name, align_bytes=64)
 
         offsets = sb.tile([P, N // 16], U16, name="offsets")
-        q_raw = [tile(f"q_raw{o}", [P, PACK, NQ], F32) for o in range(PASSES)]
+        shared = tile("vs_got_and_q_raw1", [P, N - OVERLAP + PACK * NQ], F32)
+        vs_got = shared[:, :N]
+        q_raw = [
+            tile("q_raw0", [P, PACK, NQ], F32),
+            shared[:, N - OVERLAP :].rearrange("p (t q) -> p t q", t=PACK),
+        ]
         q_rows = qT[0].rearrange("(o p t) q -> o p t q", p=P, t=PACK)
         ks_pool = tile("ks_pool", [P, T // 4], I32)
         nc.sync.dma_start(ks_pool[0:32, :], k_scales.bitcast(I32).rearrange("o r t -> r o t"))
@@ -42,13 +49,12 @@ def tile_attend_rel2_cap_topkq256n512t1024_kernel(tc, qT, k_words, k_scales, vT,
         kw_pool = tile("kw_pool", [P, T], I32)
         nc.sync.dma_start(kw_pool[:], k_words[0].rearrange("p t b -> p (t b)").bitcast(I32))
         vs_pool = tile("vs_pool", [P, T], F32)
-        nc.vector.memset(vs_pool[:, : T // 2], 0.0)
-        nc.gpsimd.memset(vs_pool[:, T // 2 :], 0.0)
-        nc.sync.dma_start(q_raw[0][:], q_rows[0])
-        nc.sync.dma_start(q_raw[1][:], q_rows[1])
-        nc.sync.dma_start(vs_pool[0:1, :], vs[0:1, :])
         nc.vector.memset(ks_pool[32:64, :], 0)
         nc.vector.memset(ks_pool[64:128, :], 0)
+        nc.vector.memset(vs_pool[:], 0.0)
+        nc.sync.dma_start(q_raw[0][:], q_rows[0])
+        nc.sync.dma_start(vs_pool[0:1, :], vs[0:1, :])
+        nc.sync.dma_start(q_raw[1][:], q_rows[1])
 
         table_in = sb.tile([P, 1], F32, name="table_in")
         table_out = sb.tile([P, 1], F32, name="table_out")
@@ -58,7 +64,8 @@ def tile_attend_rel2_cap_topkq256n512t1024_kernel(tc, qT, k_words, k_scales, vT,
         ks_planes = tile("ks_planes", [P, PASSES * N // 4], I32)
         nc.vector.memset(ks_planes[:], 0)
         ident = tile("ident", [P, P], F32)
-        make_identity(nc, ident[:])
+        nc.vector.memset(ident[:], 0.0)
+        make_identity(nc, ident[:], nomemset=True)
 
         v_pool = [tile(f"v_pool{e}", [P, T], F32) for e in range(2)]
 
@@ -96,10 +103,14 @@ def tile_attend_rel2_cap_topkq256n512t1024_kernel(tc, qT, k_words, k_scales, vT,
         def quantize(codes, scales, values):
             nc.vector.quantize_mx(out=codes.bitcast(FP8X4), scales=scales, in_=values.rearrange("p c t -> p (c t)"))
 
-        vs_got = tile("vs_got", [P, N], F32)
+        def gather_vs(lo, hi):
+            nc.vector.tensor_copy(vs_got[:, lo:hi], vs_pool[:].indirect(offsets[:, lo // 16 : hi // 16]))
+
         for o, h in both:
-            if (o, h) == both[-1]:
-                nc.vector.tensor_copy(vs_got[:], vs_pool[:].indirect(offsets[:]))
+            if (o, h) == (0, 1):
+                gather_vs(0, VS_FIRST)
+            if (o, h) == (1, 1):
+                gather_vs(VS_FIRST, N)
             quantize(q_codes[o, h][:], q_scales[o, h][:], q_bf[o][:, q_halves[h], :])
 
         vs_cols = tile("vs_cols", [P, PACK], F32)

@@ -15,13 +15,16 @@ ACT = mybir.ActivationFunctionType
 ALU = mybir.AluOpType
 
 P = 128
+QUADRANT = 32
 PACK = 4
 N, T, D, DV, NQ = 512, 1024, 1024, 256, 256
 PASSES = D // (P * PACK)
 HALVES = NQ // P
+PLANES = DV // P
+PAIRS = PACK // 2
 CAP = 2.0
+VS_FIRST = 192
 OVERLAP = 64
-VS_FIRST = 128
 
 FLOPS = 2 * NQ * N * (D + DV)
 
@@ -36,6 +39,10 @@ def tile_attend_rel2_cap_topkq256n512t1024_kernel(tc, qT, k_words, k_scales, vT,
             return sb.tile(shape, dtype, name=name, tag=tag or name, align_bytes=64)
 
         offsets = sb.tile([P, N // 16], U16, name="offsets")
+
+        def listed(lo, hi):
+            return offsets[:, lo // 16 : hi // 16]
+
         shared = tile("vs_got_and_q_raw1", [P, N - OVERLAP + PACK * NQ], F32)
         vs_got = shared[:, :N]
         q_raw = [
@@ -43,14 +50,15 @@ def tile_attend_rel2_cap_topkq256n512t1024_kernel(tc, qT, k_words, k_scales, vT,
             shared[:, N - OVERLAP :].rearrange("p (t q) -> p t q", t=PACK),
         ]
         q_rows = qT[0].rearrange("(o p t) q -> o p t q", p=P, t=PACK)
+
         ks_pool = tile("ks_pool", [P, T // 4], I32)
-        nc.sync.dma_start(ks_pool[0:32, :], k_scales.bitcast(I32).rearrange("o r t -> r o t"))
+        nc.sync.dma_start(ks_pool[:QUADRANT, :], k_scales.bitcast(I32).rearrange("o r t -> r o t"))
         nc.sync.dma_start(offsets[:], offs)
         kw_pool = tile("kw_pool", [P, T], I32)
         nc.sync.dma_start(kw_pool[:], k_words[0].rearrange("p t b -> p (t b)").bitcast(I32))
         vs_pool = tile("vs_pool", [P, T], F32)
-        nc.vector.memset(ks_pool[32:64, :], 0)
-        nc.vector.memset(ks_pool[64:128, :], 0)
+        nc.vector.memset(ks_pool[QUADRANT : 2 * QUADRANT, :], 0)
+        nc.vector.memset(ks_pool[2 * QUADRANT :, :], 0)
         nc.vector.memset(vs_pool[:], 0.0)
         nc.sync.dma_start(q_raw[0][:], q_rows[0])
         nc.sync.dma_start(vs_pool[0:1, :], vs[0:1, :])
@@ -67,155 +75,154 @@ def tile_attend_rel2_cap_topkq256n512t1024_kernel(tc, qT, k_words, k_scales, vT,
         nc.vector.memset(ident[:], 0.0)
         make_identity(nc, ident[:], nomemset=True)
 
-        v_pool = [tile(f"v_pool{e}", [P, T], F32) for e in range(2)]
+        v_pool = [tile(f"v_pool{e}", [P, T], F32) for e in range(PLANES)]
 
         ks_got = tile("ks_got", [P, N], U8)
         nc.vector.tensor_copy(ks_got[:], ks_pool[:].bitcast(U8).indirect(offsets[:]))
-        for g in range(4):
+        for g in range(P // QUADRANT):
             queue = nc.sync if g % 2 == 0 else nc.scalar
-            queue.dma_start(ks_planes[32 * g : 32 * g + 4, :], ks_got[8 * g : 8 * g + 8, :].bitcast(I32))
+            rows = ks_got[4 * PASSES * g : 4 * PASSES * (g + 1), :]
+            queue.dma_start(ks_planes[QUADRANT * g : QUADRANT * g + 4, :], rows.bitcast(I32))
         k_planes = [ks_planes[:].bitcast(U8)[:, o * N : (o + 1) * N] for o in range(PASSES)]
-        nc.sync.dma_start(v_pool[0][:], vT[:P, :])
-        nc.sync.dma_start(v_pool[1][:], vT[P:, :])
+        for e in range(PLANES):
+            nc.sync.dma_start(v_pool[e][:], vT[e * P : (e + 1) * P, :])
+
         kw_got = tile("kw_got", [P, N], U32)
-        slot_halves = [slice(c * N // 2, (c + 1) * N // 2) for c in range(2)]
-        for c, cols in enumerate(slot_halves):
-            listed = offsets[:, c * N // 32 : (c + 1) * N // 32]
-            nc.vector.tensor_copy(kw_got[:, cols], kw_pool[:].bitcast(U32).indirect(listed))
+        slot_halves = [slice(0, N // 2), slice(N // 2, N)]
+        for cols in slot_halves:
+            nc.vector.tensor_copy(kw_got[:, cols], kw_pool[:].bitcast(U32).indirect(listed(cols.start, cols.stop)))
         k_codes = tile("k_codes", [P, PASSES, N], U16)
         for cols in slot_halves:
             nc.vector.tensor_copy(
                 k_codes[:, :, cols], kw_got[:, cols].bitcast(U16).rearrange("p (i o) -> p o i", o=PASSES)
             )
 
-        both = [(o, h) for o in range(PASSES) for h in range(HALVES)]
+        pass_half = [(o, h) for o in range(PASSES) for h in range(HALVES)]
         q_bf = [tile(f"q_bf{o}", [P, NQ, PACK], BF16) for o in range(PASSES)]
-        q_codes = {(o, h): tile(f"q_codes{o}{h}", [P, P], U32) for o, h in both}
-        q_scales = {(o, h): tile(f"q_scales{o}{h}", [P, P], U8) for o, h in both}
+        q_codes = {(o, h): tile(f"q_codes{o}{h}", [P, P], U32) for o, h in pass_half}
+        q_scales = {(o, h): tile(f"q_scales{o}{h}", [P, P], U8) for o, h in pass_half}
         q_halves = [slice(h * P, (h + 1) * P) for h in range(HALVES)]
-        for o, h in both:
+        for o, h in pass_half:
             nc.scalar.activation(
-                q_bf[o][:, q_halves[h], :].rearrange("p (c i) t -> p c t i", i=4),
-                q_raw[o][:, :, h * P : (h + 1) * P].rearrange("p t (c i) -> p c t i", i=4),
+                q_bf[o][:, q_halves[h], :].rearrange("p (a b) t -> p a t b", b=4),
+                q_raw[o][:, :, q_halves[h]].rearrange("p t (a b) -> p a t b", b=4),
                 ACT.Copy,
             )
 
         def quantize(codes, scales, values):
-            nc.vector.quantize_mx(out=codes.bitcast(FP8X4), scales=scales, in_=values.rearrange("p c t -> p (c t)"))
+            nc.vector.quantize_mx(out=codes.bitcast(FP8X4), scales=scales, in_=values.rearrange("p x t -> p (x t)"))
 
-        def gather_vs(lo, hi):
-            nc.vector.tensor_copy(vs_got[:, lo:hi], vs_pool[:].indirect(offsets[:, lo // 16 : hi // 16]))
-
-        for o, h in both:
-            if (o, h) == (0, 1):
-                gather_vs(0, VS_FIRST)
-            if (o, h) == (1, 1):
-                gather_vs(VS_FIRST, N)
+        vs_pieces = [(0, VS_FIRST), (VS_FIRST, N)]
+        for o, h in pass_half:
+            if h == 1:
+                lo, hi = vs_pieces[o]
+                nc.vector.tensor_copy(vs_got[:, lo:hi], vs_pool[:].indirect(listed(lo, hi)))
             quantize(q_codes[o, h][:], q_scales[o, h][:], q_bf[o][:, q_halves[h], :])
 
         vs_cols = tile("vs_cols", [P, PACK], F32)
         nc.sync.dma_start(vs_cols[:], vs_got[0:1, :])
 
         scores = [ps.tile([P, N], F32, name=f"scores{h}", tag=f"scores{h}") for h in range(HALVES)]
-        for h, o in both:
-            nc.tensor.matmul_mx(
-                out=scores[h][:],
-                lhsT=q_codes[o, h][:].bitcast(FP8X4),
-                lhsT_scale=q_scales[o, h][:],
-                rhs=k_codes[:, o, :].bitcast(FP4X4),
-                rhs_scale=k_planes[o],
-                start=(o == 0),
-                stop=(o == PASSES - 1),
-            )
+        for h in range(HALVES):
+            for o in range(PASSES):
+                nc.tensor.matmul_mx(
+                    out=scores[h][:],
+                    lhsT=q_codes[o, h][:].bitcast(FP8X4),
+                    lhsT_scale=q_scales[o, h][:],
+                    rhs=k_codes[:, o, :].bitcast(FP4X4),
+                    rhs_scale=k_planes[o],
+                    start=(o == 0),
+                    stop=(o == PASSES - 1),
+                )
 
-        v_got = [tile(f"v_got{e}", [P, N], BF16) for e in range(2)]
-        for e in range(2):
+        v_got = [tile(f"v_got{e}", [P, N], BF16) for e in range(PLANES)]
+        for e in range(PLANES):
             nc.vector.tensor_copy(v_got[e][:], v_pool[e][:].indirect(offsets[:]))
 
-        th = [tile(f"th{h}", [P, N], F32) for h in range(HALVES)]
+        half_pair = [(h, c) for h in range(HALVES) for c in range(PAIRS)]
+        capped = [tile(f"capped{h}", [P, N], F32) for h in range(HALVES)]
         positive = [tile(f"positive{h}", [P, N], F32) for h in range(HALVES)]
-        pq = [tile(f"pq{h}", [P, N], F32) for h in range(HALVES)]
-        sums = tile("sums", [P, 2 * HALVES], F32)
+        squares = {(h, c): tile(f"squares{h}{c}", [P, N // PAIRS], F32) for h, c in half_pair}
+        sums = tile("sums", [P, HALVES * PAIRS], F32)
         p_turned = [ps.tile([P, PACK, P], F32, name=f"p_turned{h}") for h in range(HALVES)]
         w_bf = [tile(f"w_bf{h}", [P, P, PACK], BF16) for h in range(HALVES)]
         w_scales = [tile(f"w_scales{h}", [P, P], U8) for h in range(HALVES)]
-        pair_cols = [slice(c * N // 2, (c + 1) * N // 2) for c in range(2)]
+        pair_cols = [slice(c * N // PAIRS, (c + 1) * N // PAIRS) for c in range(PAIRS)]
 
-        def turn(bank, source):
-            for t in range(PACK):
-                nc.tensor.transpose(bank[:, t, :], source[:, t * P : (t + 1) * P], ident[:])
+        def sum_of(h, c):
+            return sums[:, PAIRS * h + c : PAIRS * h + c + 1]
 
         def cap(h, c):
             nc.scalar.activation(
-                th[h][:, pair_cols[c]].rearrange("p (t s) -> p t s", t=2),
+                capped[h][:, pair_cols[c]].rearrange("p (t s) -> p t s", t=2),
                 scores[h][:].rearrange("p (s t) -> p t s", t=PACK)[:, 2 * c : 2 * c + 2],
                 ACT.Tanh,
                 scale=1.0 / CAP,
             )
 
-        def clamp(h, c):
-            nc.gpsimd.tensor_scalar(positive[h][:, pair_cols[c]], th[h][:, pair_cols[c]], 1.0, 0.0, ALU.min, ALU.max)
+        def clamp_on_gpsimd(h, c):
+            cols = pair_cols[c]
+            nc.gpsimd.tensor_scalar(positive[h][:, cols], capped[h][:, cols], 1.0, 0.0, ALU.min, ALU.max)
 
-        def square(h, c):
-            nc.scalar.activation(
-                pq[h][:, pair_cols[c]],
-                positive[h][:, pair_cols[c]],
-                ACT.Square,
-                accum_out=sums[:, 2 * h + c : 2 * h + c + 1],
+        def clamp_on_scalar(h, c):
+            nc.scalar.activation(positive[h][:, pair_cols[c]], capped[h][:, pair_cols[c]], ACT.Relu)
+
+        def square_on_scalar(h, c):
+            nc.scalar.activation(squares[h, c][:], positive[h][:, pair_cols[c]], ACT.Square, accum_out=sum_of(h, c))
+
+        def clamp_and_square_on_vector(h, c):
+            nc.vector.scalar_tensor_tensor(
+                out=squares[h, c][:],
+                in0=capped[h][:, pair_cols[c]],
+                scalar=0.0,
+                in1=capped[h][:, pair_cols[c]],
+                op0=ALU.max,
+                op1=ALU.mult,
+                accum_out=sum_of(h, c),
             )
 
-        v_bf = [tile("v_bf0", [P, P, PACK], BF16, tag="positive1"), tile("v_bf1", [P, P, PACK], BF16)]
+        def turn_squares(h):
+            for t in range(PACK):
+                source = squares[h, t // 2][:, t % 2 * P : (t % 2 + 1) * P]
+                nc.tensor.transpose(p_turned[h][:, t, :], source, ident[:])
 
-        def turn_values(e, tag):
-            bank = ps.tile([P, 2, P], F32, name=f"v_turned{e}", tag=tag)
+        v_bf = [tile("v_bf0", [P, P, PACK], BF16, tag="positive0"), tile("v_bf1", [P, P, PACK], BF16)]
+
+        def turn_values(e):
+            bank = ps.tile([P, PAIRS, P], F32, name=f"v_turned{e}", tag=f"scores{e}")
             words = v_got[e][:].bitcast(F32)
-            for c in range(2):
-                nc.tensor.transpose(bank[:, c, :], words[:, c : N // 2 : 2], ident[:])
+            for c in range(PAIRS):
+                nc.tensor.transpose(bank[:, c, :], words[:, c : N // 2 : PAIRS], ident[:])
             nc.scalar.copy(
-                v_bf[e][:].rearrange("p f t -> p (f t)").bitcast(F32).rearrange("p (f c) -> p f c", c=2),
+                v_bf[e][:].rearrange("p f t -> p (f t)").bitcast(F32).rearrange("p (f c) -> p f c", c=PAIRS),
                 bank[:].rearrange("p c f -> p f c"),
             )
 
         cap(0, 1)
         cap(0, 0)
-        clamp(0, 0)
-        nc.scalar.activation(positive[0][:, pair_cols[1]], th[0][:, pair_cols[1]], ACT.Relu)
+        clamp_on_gpsimd(0, 0)
+        clamp_on_scalar(0, 1)
         cap(1, 0)
-        clamp(1, 0)
-        square(0, 1)
-        square(0, 0)
+        clamp_on_gpsimd(1, 0)
+        square_on_scalar(0, 1)
+        square_on_scalar(0, 0)
         cap(1, 1)
-        turn(p_turned[0], pq[0][:])
-        square(1, 0)
-        nc.vector.scalar_tensor_tensor(
-            out=pq[1][:, pair_cols[1]],
-            in0=th[1][:, pair_cols[1]],
-            scalar=0.0,
-            in1=th[1][:, pair_cols[1]],
-            op0=ALU.max,
-            op1=ALU.mult,
-            accum_out=sums[:, 3:4],
-        )
-        turn_values(0, "scores0")
-        turn(p_turned[1], pq[1][:])
-        turn_values(1, "scores1")
+        turn_squares(0)
+        turn_values(0)
+        square_on_scalar(1, 0)
+        clamp_and_square_on_vector(1, 1)
+        turn_squares(1)
+        turn_values(1)
 
-        totals = tile("totals", [P, HALVES], F32)
+        totals = [tile(f"totals{h}", [P, 1], F32) for h in range(HALVES)]
+        inverse = [tile(f"inverse{h}", [P, 1], F32) for h in range(HALVES)]
         for h in range(HALVES):
-            nc.gpsimd.tensor_scalar(
-                totals[:, h : h + 1],
-                sums[:, 2 * h : 2 * h + 1],
-                sums[:, 2 * h + 1 : 2 * h + 2],
-                1.0 / (CAP * CAP),
-                ALU.add,
-                ALU.add,
-            )
+            nc.gpsimd.tensor_scalar(totals[h][:], sum_of(h, 0), sum_of(h, 1), 1.0 / (CAP * CAP), ALU.add, ALU.add)
 
-        e_halves = [slice(0, P), slice(P, DV)]
-        v_codes = [tile(f"v_codes{e}", [P, P], U32, tag=f"pq{e}") for e in range(2)]
-        v_scales = [tile(f"v_scales{e}", [P, P], U8) for e in range(2)]
+        v_codes = [tile(f"v_codes{e}", [P, P], U32, tag=f"squares{e}1") for e in range(PLANES)]
+        v_scales = [tile(f"v_scales{e}", [P, P], U8) for e in range(PLANES)]
         w_codes = [tile(f"w_codes{h}", [P, P], U32) for h in range(HALVES)]
-        for x in range(2):
+        for x in range(HALVES):
             nc.vector.tensor_tensor(
                 out=w_bf[x][:],
                 in0=p_turned[x][:].rearrange("p t q -> p q t"),
@@ -224,12 +231,10 @@ def tile_attend_rel2_cap_topkq256n512t1024_kernel(tc, qT, k_words, k_scales, vT,
             )
             quantize(v_codes[x][:], v_scales[x][:], v_bf[x][:])
             quantize(w_codes[x][:], w_scales[x][:], w_bf[x][:])
-            if x == 0:
-                inverse = tile("inverse", [P, HALVES], F32)
-                nc.vector.reciprocal(inverse[:], totals[:])
+            nc.vector.reciprocal(inverse[x][:], totals[x][:])
 
         for h in range(HALVES):
-            for e, cols in enumerate(e_halves):
+            for e in range(PLANES):
                 acc = ps.tile([P, P], F32, name=f"acc{h}{e}")
                 nc.tensor.matmul_mx(
                     out=acc[:],
@@ -241,9 +246,10 @@ def tile_attend_rel2_cap_topkq256n512t1024_kernel(tc, qT, k_words, k_scales, vT,
                     stop=True,
                 )
                 y = tile(f"y{h}{e}", [P, P], F32)
-                if (h, e) == (1, 0):
-                    nc.vector.tensor_scalar(y[:], acc[:], inverse[:, h : h + 1], None, ALU.mult)
+                last_half = h == HALVES - 1
+                if last_half and e == 0:
+                    nc.vector.tensor_scalar(y[:], acc[:], inverse[h][:], None, ALU.mult)
                 else:
-                    nc.scalar.activation(y[:], acc[:], ACT.Copy, scale=inverse[:, h : h + 1])
-                queue = nc.scalar if (h, e) == (1, 1) else nc.sync
-                queue.dma_start(out[0, q_halves[h], cols], y[:])
+                    nc.scalar.activation(y[:], acc[:], ACT.Copy, scale=inverse[h][:])
+                queue = nc.scalar if last_half and e == 1 else nc.sync
+                queue.dma_start(out[0, q_halves[h], e * P : (e + 1) * P], y[:])

@@ -23,8 +23,7 @@ HALVES = NQ // P
 PLANES = DV // P
 PAIRS = PACK // 2
 CAP = 2.0
-VS_FIRST = 192
-OVERLAP = 64
+V_AHEAD = 384
 
 FLOPS = 2 * NQ * N * (D + DV)
 
@@ -43,26 +42,21 @@ def tile_attend_rel2_cap_topkq256n512t1024_kernel(tc, qT, k_words, k_scales, vT,
         def listed(lo, hi):
             return offsets[:, lo // 16 : hi // 16]
 
-        shared = tile("vs_got_and_q_raw1", [P, N - OVERLAP + PACK * NQ], F32)
-        vs_got = shared[:, :N]
-        q_raw = [
-            tile("q_raw0", [P, PACK, NQ], F32),
-            shared[:, N - OVERLAP :].rearrange("p (t q) -> p t q", t=PACK),
-        ]
         q_rows = qT[0].rearrange("(o p t) q -> o p t q", p=P, t=PACK)
+        q_raw = [tile(f"q_raw{o}", [P, PACK, NQ], F32) for o in range(PASSES)]
 
+        vs_pool = tile("vs_pool", [P, T], F32)
+        nc.vector.memset(vs_pool[:], 0.0)
         ks_pool = tile("ks_pool", [P, T // 4], I32)
         nc.sync.dma_start(ks_pool[:QUADRANT, :], k_scales.bitcast(I32).rearrange("o r t -> r o t"))
         nc.sync.dma_start(offsets[:], offs)
         kw_pool = tile("kw_pool", [P, T], I32)
         nc.sync.dma_start(kw_pool[:], k_words[0].rearrange("p t b -> p (t b)").bitcast(I32))
-        vs_pool = tile("vs_pool", [P, T], F32)
+        nc.sync.dma_start(vs_pool[0:1, :], vs[0:1, :])
         nc.vector.memset(ks_pool[QUADRANT : 2 * QUADRANT, :], 0)
         nc.vector.memset(ks_pool[2 * QUADRANT :, :], 0)
-        nc.vector.memset(vs_pool[:], 0.0)
-        nc.sync.dma_start(q_raw[0][:], q_rows[0])
-        nc.sync.dma_start(vs_pool[0:1, :], vs[0:1, :])
-        nc.sync.dma_start(q_raw[1][:], q_rows[1])
+        for o in range(PASSES):
+            nc.sync.dma_start(q_raw[o][:], q_rows[o])
 
         table_in = sb.tile([P, 1], F32, name="table_in")
         table_out = sb.tile([P, 1], F32, name="table_out")
@@ -77,20 +71,29 @@ def tile_attend_rel2_cap_topkq256n512t1024_kernel(tc, qT, k_words, k_scales, vT,
 
         v_pool = [tile(f"v_pool{e}", [P, T], F32) for e in range(PLANES)]
 
+        nc.sync.dma_start(v_pool[0][:, :V_AHEAD], vT[0:P, :V_AHEAD])
+
+        vs_got = tile("vs_got", [P, N], F32)
+        nc.scalar.activation(vs_got[:], vs_pool[:].indirect(offsets[:]), ACT.Copy)
+
         ks_got = tile("ks_got", [P, N], U8)
         nc.vector.tensor_copy(ks_got[:], ks_pool[:].bitcast(U8).indirect(offsets[:]))
         for g in range(P // QUADRANT):
-            queue = nc.sync if g % 2 == 0 else nc.scalar
             rows = ks_got[4 * PASSES * g : 4 * PASSES * (g + 1), :]
-            queue.dma_start(ks_planes[QUADRANT * g : QUADRANT * g + 4, :], rows.bitcast(I32))
+            nc.sync.dma_start(ks_planes[QUADRANT * g : QUADRANT * g + 4, :], rows.bitcast(I32))
         k_planes = [ks_planes[:].bitcast(U8)[:, o * N : (o + 1) * N] for o in range(PASSES)]
-        for e in range(PLANES):
-            nc.sync.dma_start(v_pool[e][:], vT[e * P : (e + 1) * P, :])
+        nc.sync.dma_start(v_pool[0][:, V_AHEAD:], vT[0:P, V_AHEAD:])
+        nc.sync.dma_start(v_pool[1][:], vT[P : 2 * P, :])
+        vs_cols = tile("vs_cols", [P, PACK], F32)
+
+        nc.sync.dma_start(vs_cols[:], vs_got[0:1, :])
 
         kw_got = tile("kw_got", [P, N], U32)
         slot_halves = [slice(0, N // 2), slice(N // 2, N)]
         for cols in slot_halves:
-            nc.vector.tensor_copy(kw_got[:, cols], kw_pool[:].bitcast(U32).indirect(listed(cols.start, cols.stop)))
+            nc.vector.tensor_copy(
+                kw_got[:, cols], kw_pool[:].bitcast(U32).indirect(offsets[:, cols.start // 16 : cols.stop // 16])
+            )
         k_codes = tile("k_codes", [P, PASSES, N], U16)
         for cols in slot_halves:
             nc.vector.tensor_copy(
@@ -98,95 +101,81 @@ def tile_attend_rel2_cap_topkq256n512t1024_kernel(tc, qT, k_words, k_scales, vT,
             )
 
         pass_half = [(o, h) for o in range(PASSES) for h in range(HALVES)]
-        q_bf = [tile(f"q_bf{o}", [P, NQ, PACK], BF16) for o in range(PASSES)]
+        q_bf = {(o, h): tile(f"q_bf{o}{h}", [P, P, PACK], BF16) for o, h in pass_half}
         q_codes = {(o, h): tile(f"q_codes{o}{h}", [P, P], U32) for o, h in pass_half}
         q_scales = {(o, h): tile(f"q_scales{o}{h}", [P, P], U8) for o, h in pass_half}
         q_halves = [slice(h * P, (h + 1) * P) for h in range(HALVES)]
-        for o, h in pass_half:
-            nc.scalar.activation(
-                q_bf[o][:, q_halves[h], :].rearrange("p (a b) t -> p a t b", b=4),
-                q_raw[o][:, :, q_halves[h]].rearrange("p t (a b) -> p a t b", b=4),
-                ACT.Copy,
-            )
+
+        def cast(o, h, on_vector):
+            dst = q_bf[o, h][:].rearrange("p (a b) t -> p a t b", b=4)
+            src = q_raw[o][:, :, q_halves[h]].rearrange("p t (a b) -> p a t b", b=4)
+            if on_vector:
+                nc.vector.tensor_copy(dst, src)
+            else:
+                nc.scalar.activation(dst, src, ACT.Copy)
 
         def quantize(codes, scales, values):
             nc.vector.quantize_mx(out=codes.bitcast(FP8X4), scales=scales, in_=values.rearrange("p x t -> p (x t)"))
 
-        vs_pieces = [(0, VS_FIRST), (VS_FIRST, N)]
-        for o, h in pass_half:
-            if h == 1:
-                lo, hi = vs_pieces[o]
-                nc.vector.tensor_copy(vs_got[:, lo:hi], vs_pool[:].indirect(listed(lo, hi)))
-            quantize(q_codes[o, h][:], q_scales[o, h][:], q_bf[o][:, q_halves[h], :])
+        def quantize_q(o, h):
+            quantize(q_codes[o, h][:], q_scales[o, h][:], q_bf[o, h][:])
 
-        vs_cols = tile("vs_cols", [P, PACK], F32)
-        nc.sync.dma_start(vs_cols[:], vs_got[0:1, :])
+        cast(0, 0, False)
+        cast(0, 1, False)
+        cast(1, 0, True)
+        quantize_q(0, 0)
+        cast(1, 1, False)
+        quantize_q(1, 0)
+        quantize_q(0, 1)
+        quantize_q(1, 1)
 
         scores = [ps.tile([P, N], F32, name=f"scores{h}", tag=f"scores{h}") for h in range(HALVES)]
-        for h in range(HALVES):
-            for o in range(PASSES):
-                nc.tensor.matmul_mx(
-                    out=scores[h][:],
-                    lhsT=q_codes[o, h][:].bitcast(FP8X4),
-                    lhsT_scale=q_scales[o, h][:],
-                    rhs=k_codes[:, o, :].bitcast(FP4X4),
-                    rhs_scale=k_planes[o],
-                    start=(o == 0),
-                    stop=(o == PASSES - 1),
-                )
+        for h, o in pass_half:
+            nc.tensor.matmul_mx(
+                out=scores[h][:],
+                lhsT=q_codes[o, h][:].bitcast(FP8X4),
+                lhsT_scale=q_scales[o, h][:],
+                rhs=k_codes[:, o, :].bitcast(FP4X4),
+                rhs_scale=k_planes[o],
+                start=(o == 0),
+                stop=(o == PASSES - 1),
+            )
 
-        v_got = [tile(f"v_got{e}", [P, N], BF16) for e in range(PLANES)]
-        for e in range(PLANES):
-            nc.vector.tensor_copy(v_got[e][:], v_pool[e][:].indirect(offsets[:]))
+        v_got = [tile("v_got0", [P, N], BF16), tile("v_got1", [P, N], BF16)]
+        nc.vector.tensor_copy(v_got[0][:], v_pool[0][:].indirect(offsets[:]))
 
         half_pair = [(h, c) for h in range(HALVES) for c in range(PAIRS)]
-        capped = [tile(f"capped{h}", [P, N], F32) for h in range(HALVES)]
-        positive = [tile(f"positive{h}", [P, N], F32) for h in range(HALVES)]
-        squares = {(h, c): tile(f"squares{h}{c}", [P, N // PAIRS], F32) for h, c in half_pair}
+        capped = {(h, c): tile(f"capped{h}{c}", [P, N // PAIRS], F32) for h, c in half_pair}
+        squares = {
+            (h, c): tile(f"squares{h}{c}", [P, N // PAIRS], F32, tag="v_pool0" if h + c == 0 else None)
+            for h, c in half_pair
+        }
         sums = tile("sums", [P, HALVES * PAIRS], F32)
         p_turned = [ps.tile([P, PACK, P], F32, name=f"p_turned{h}") for h in range(HALVES)]
         w_bf = [tile(f"w_bf{h}", [P, P, PACK], BF16) for h in range(HALVES)]
         w_scales = [tile(f"w_scales{h}", [P, P], U8) for h in range(HALVES)]
-        pair_cols = [slice(c * N // PAIRS, (c + 1) * N // PAIRS) for c in range(PAIRS)]
 
         def sum_of(h, c):
             return sums[:, PAIRS * h + c : PAIRS * h + c + 1]
 
         def cap(h, c):
             nc.scalar.activation(
-                capped[h][:, pair_cols[c]].rearrange("p (t s) -> p t s", t=2),
+                capped[h, c][:].rearrange("p (t s) -> p t s", t=2),
                 scores[h][:].rearrange("p (s t) -> p t s", t=PACK)[:, 2 * c : 2 * c + 2],
                 ACT.Tanh,
                 scale=1.0 / CAP,
             )
 
-        def clamp_on_gpsimd(h, c):
-            cols = pair_cols[c]
-            nc.gpsimd.tensor_scalar(positive[h][:, cols], capped[h][:, cols], 1.0, 0.0, ALU.min, ALU.max)
+        def gather_on_scalar(lo, hi):
+            nc.scalar.activation(v_got[1][:, lo:hi], v_pool[1][:].indirect(listed(lo, hi)), ACT.Copy)
 
-        def clamp_on_scalar(h, c):
-            nc.scalar.activation(positive[h][:, pair_cols[c]], capped[h][:, pair_cols[c]], ACT.Relu)
+        cap(0, 0)
+        cap(0, 1)
+        cap(1, 0)
+        cap(1, 1)
+        gather_on_scalar(0, N)
 
-        def square_on_scalar(h, c):
-            nc.scalar.activation(squares[h, c][:], positive[h][:, pair_cols[c]], ACT.Square, accum_out=sum_of(h, c))
-
-        def clamp_and_square_on_vector(h, c):
-            nc.vector.scalar_tensor_tensor(
-                out=squares[h, c][:],
-                in0=capped[h][:, pair_cols[c]],
-                scalar=0.0,
-                in1=capped[h][:, pair_cols[c]],
-                op0=ALU.max,
-                op1=ALU.mult,
-                accum_out=sum_of(h, c),
-            )
-
-        def turn_squares(h):
-            for t in range(PACK):
-                source = squares[h, t // 2][:, t % 2 * P : (t % 2 + 1) * P]
-                nc.tensor.transpose(p_turned[h][:, t, :], source, ident[:])
-
-        v_bf = [tile("v_bf0", [P, P, PACK], BF16, tag="positive0"), tile("v_bf1", [P, P, PACK], BF16)]
+        v_bf = [tile("v_bf0", [P, P, PACK], BF16, tag="v_pool1"), tile("v_bf1", [P, P, PACK], BF16)]
 
         def turn_values(e):
             bank = ps.tile([P, PAIRS, P], F32, name=f"v_turned{e}", tag=f"scores{e}")
@@ -198,43 +187,49 @@ def tile_attend_rel2_cap_topkq256n512t1024_kernel(tc, qT, k_words, k_scales, vT,
                 bank[:].rearrange("p c f -> p f c"),
             )
 
-        cap(0, 1)
-        cap(0, 0)
-        clamp_on_gpsimd(0, 0)
-        clamp_on_scalar(0, 1)
-        cap(1, 0)
-        clamp_on_gpsimd(1, 0)
-        square_on_scalar(0, 1)
-        square_on_scalar(0, 0)
-        cap(1, 1)
-        turn_squares(0)
         turn_values(0)
-        square_on_scalar(1, 0)
-        clamp_and_square_on_vector(1, 1)
-        turn_squares(1)
+        for h, c in half_pair:
+            nc.vector.scalar_tensor_tensor(
+                out=squares[h, c][:],
+                in0=capped[h, c][:],
+                scalar=0.0,
+                in1=capped[h, c][:],
+                op0=ALU.max,
+                op1=ALU.mult,
+                accum_out=sum_of(h, c),
+            )
+            for t in range(2):
+                nc.tensor.transpose(p_turned[h][:, 2 * c + t, :], squares[h, c][:, t * P : (t + 1) * P], ident[:])
         turn_values(1)
 
-        totals = [tile(f"totals{h}", [P, 1], F32) for h in range(HALVES)]
-        inverse = [tile(f"inverse{h}", [P, 1], F32) for h in range(HALVES)]
-        for h in range(HALVES):
-            nc.gpsimd.tensor_scalar(totals[h][:], sum_of(h, 0), sum_of(h, 1), 1.0 / (CAP * CAP), ALU.add, ALU.add)
+        totals = tile("totals", [P, HALVES], F32)
+        inverse = tile("inverse", [P, HALVES], F32)
+        pairs_of = sums[:].rearrange("p (h c) -> p h c", c=PAIRS)
+        nc.vector.scalar_tensor_tensor(
+            out=totals[:], in0=pairs_of[:, :, 0], scalar=1.0 / (CAP * CAP), in1=pairs_of[:, :, 1], op0=ALU.add, op1=ALU.add
+        )
 
-        v_codes = [tile(f"v_codes{e}", [P, P], U32, tag=f"squares{e}1") for e in range(PLANES)]
+        v_codes = [tile("v_codes0", [P, P], U32), tile("v_codes1", [P, P], U32, tag="vs_cols")]
         v_scales = [tile(f"v_scales{e}", [P, P], U8) for e in range(PLANES)]
         w_codes = [tile(f"w_codes{h}", [P, P], U32) for h in range(HALVES)]
-        for x in range(HALVES):
+
+        def weigh(h):
             nc.vector.tensor_tensor(
-                out=w_bf[x][:],
-                in0=p_turned[x][:].rearrange("p t q -> p q t"),
+                out=w_bf[h][:],
+                in0=p_turned[h][:].rearrange("p t q -> p q t"),
                 in1=vs_cols[:].unsqueeze(1).broadcast_to([P, P, PACK]),
                 op=ALU.mult,
             )
-            quantize(v_codes[x][:], v_scales[x][:], v_bf[x][:])
-            quantize(w_codes[x][:], w_scales[x][:], w_bf[x][:])
-            nc.vector.reciprocal(inverse[x][:], totals[x][:])
 
-        for h in range(HALVES):
-            for e in range(PLANES):
+        weigh(0)
+        nc.vector.reciprocal(inverse[:], totals[:])
+        weigh(1)
+        for x in range(HALVES):
+            quantize(w_codes[x][:], w_scales[x][:], w_bf[x][:])
+            quantize(v_codes[x][:], v_scales[x][:], v_bf[x][:])
+
+        for e in range(PLANES):
+            for h in range(HALVES):
                 acc = ps.tile([P, P], F32, name=f"acc{h}{e}")
                 nc.tensor.matmul_mx(
                     out=acc[:],
@@ -246,10 +241,10 @@ def tile_attend_rel2_cap_topkq256n512t1024_kernel(tc, qT, k_words, k_scales, vT,
                     stop=True,
                 )
                 y = tile(f"y{h}{e}", [P, P], F32)
-                last_half = h == HALVES - 1
-                if last_half and e == 0:
-                    nc.vector.tensor_scalar(y[:], acc[:], inverse[h][:], None, ALU.mult)
+                last_plane = e == PLANES - 1
+                if last_plane and h == 0:
+                    nc.vector.tensor_scalar(y[:], acc[:], inverse[:, h : h + 1], None, ALU.mult)
                 else:
-                    nc.scalar.activation(y[:], acc[:], ACT.Copy, scale=inverse[h][:])
-                queue = nc.scalar if last_half and e == 1 else nc.sync
+                    nc.scalar.activation(y[:], acc[:], ACT.Copy, scale=inverse[:, h : h + 1])
+                queue = nc.scalar if last_plane and h == 1 else nc.sync
                 queue.dma_start(out[0, q_halves[h], e * P : (e + 1) * P], y[:])

@@ -24,6 +24,7 @@ PLANES = DV // P
 PAIRS = PACK // 2
 CAP = 2.0
 V_AHEAD = 384
+V_SPLIT = 224
 
 FLOPS = 2 * NQ * N * (D + DV)
 
@@ -77,16 +78,17 @@ def tile_attend_rel2_cap_topkq256n512t1024_kernel(tc, qT, k_words, k_scales, vT,
         nc.scalar.activation(vs_got[:], vs_pool[:].indirect(offsets[:]), ACT.Copy)
 
         ks_got = tile("ks_got", [P, N], U8)
-        nc.vector.tensor_copy(ks_got[:], ks_pool[:].bitcast(U8).indirect(offsets[:]))
+        nc.vector.tensor_copy(
+            ks_got[:].rearrange("p (c s e) -> p s c e", c=PAIRS, e=2), ks_pool[:].bitcast(U8).indirect(offsets[:])
+        )
         for g in range(P // QUADRANT):
             rows = ks_got[4 * PASSES * g : 4 * PASSES * (g + 1), :]
             nc.sync.dma_start(ks_planes[QUADRANT * g : QUADRANT * g + 4, :], rows.bitcast(I32))
         k_planes = [ks_planes[:].bitcast(U8)[:, o * N : (o + 1) * N] for o in range(PASSES)]
         nc.sync.dma_start(v_pool[0][:, V_AHEAD:], vT[0:P, V_AHEAD:])
-        nc.sync.dma_start(v_pool[1][:], vT[P : 2 * P, :])
         vs_cols = tile("vs_cols", [P, PACK], F32)
-
         nc.sync.dma_start(vs_cols[:], vs_got[0:1, :])
+        nc.sync.dma_start(v_pool[1][:], vT[P : 2 * P, :])
 
         kw_got = tile("kw_got", [P, N], U32)
         slot_halves = [slice(0, N // 2), slice(N // 2, N)]
@@ -95,10 +97,11 @@ def tile_attend_rel2_cap_topkq256n512t1024_kernel(tc, qT, k_words, k_scales, vT,
                 kw_got[:, cols], kw_pool[:].bitcast(U32).indirect(offsets[:, cols.start // 16 : cols.stop // 16])
             )
         k_codes = tile("k_codes", [P, PASSES, N], U16)
-        for cols in slot_halves:
-            nc.vector.tensor_copy(
-                k_codes[:, :, cols], kw_got[:, cols].bitcast(U16).rearrange("p (i o) -> p o i", o=PASSES)
-            )
+        dealt = k_codes[:].rearrange("p o (c s e) -> p o s c e", c=PAIRS, e=2)
+        listed_words = kw_got[:].bitcast(U16).rearrange("p (s c e o) -> p o s c e", c=PAIRS, e=2, o=PASSES)
+        for x in range(2):
+            rows = slice(x * P // 2, (x + 1) * P // 2)
+            nc.vector.tensor_copy(dealt[:, :, rows], listed_words[:, :, rows])
 
         pass_half = [(o, h) for o in range(PASSES) for h in range(HALVES)]
         q_bf = {(o, h): tile(f"q_bf{o}{h}", [P, P, PACK], BF16) for o, h in pass_half}
@@ -129,27 +132,28 @@ def tile_attend_rel2_cap_topkq256n512t1024_kernel(tc, qT, k_words, k_scales, vT,
         quantize_q(0, 1)
         quantize_q(1, 1)
 
-        scores = [ps.tile([P, N], F32, name=f"scores{h}", tag=f"scores{h}") for h in range(HALVES)]
-        for h, o in pass_half:
-            nc.tensor.matmul_mx(
-                out=scores[h][:],
-                lhsT=q_codes[o, h][:].bitcast(FP8X4),
-                lhsT_scale=q_scales[o, h][:],
-                rhs=k_codes[:, o, :].bitcast(FP4X4),
-                rhs_scale=k_planes[o],
-                start=(o == 0),
-                stop=(o == PASSES - 1),
-            )
+        half_pair = [(h, c) for h in range(HALVES) for c in range(PAIRS)]
+        pair_cols = [slice(c * N // PAIRS, (c + 1) * N // PAIRS) for c in range(PAIRS)]
+        scores = {(h, c): ps.tile([P, N // PAIRS], F32, name=f"scores{h}{c}", tag=f"scores{h}{c}") for h, c in half_pair}
+        for h, c in half_pair:
+            for o in range(PASSES):
+                nc.tensor.matmul_mx(
+                    out=scores[h, c][:],
+                    lhsT=q_codes[o, h][:].bitcast(FP8X4),
+                    lhsT_scale=q_scales[o, h][:],
+                    rhs=k_codes[:, o, pair_cols[c]].bitcast(FP4X4),
+                    rhs_scale=k_planes[o][:, pair_cols[c]],
+                    start=(o == 0),
+                    stop=(o == PASSES - 1),
+                )
 
         v_got = [tile("v_got0", [P, N], BF16), tile("v_got1", [P, N], BF16)]
-        nc.vector.tensor_copy(v_got[0][:], v_pool[0][:].indirect(offsets[:]))
+        nc.scalar.activation(v_got[0][:, :V_SPLIT], v_pool[0][:].indirect(listed(0, V_SPLIT)), ACT.Copy)
+        nc.vector.tensor_copy(v_got[0][:, V_SPLIT:], v_pool[0][:].indirect(listed(V_SPLIT, N)))
 
-        half_pair = [(h, c) for h in range(HALVES) for c in range(PAIRS)]
-        capped = {(h, c): tile(f"capped{h}{c}", [P, N // PAIRS], F32) for h, c in half_pair}
-        squares = {
-            (h, c): tile(f"squares{h}{c}", [P, N // PAIRS], F32, tag="v_pool0" if h + c == 0 else None)
-            for h, c in half_pair
-        }
+        capped_all = tile("capped", [P, HALVES, N], F32, tag="vs_got")
+        capped = {(h, c): capped_all[:, h, pair_cols[c]] for h, c in half_pair}
+        squares = {(h, c): tile(f"squares{h}{c}", [P, N // PAIRS], F32) for h, c in half_pair}
         sums = tile("sums", [P, HALVES * PAIRS], F32)
         p_turned = [ps.tile([P, PACK, P], F32, name=f"p_turned{h}") for h in range(HALVES)]
         w_bf = [tile(f"w_bf{h}", [P, P, PACK], BF16) for h in range(HALVES)]
@@ -160,8 +164,8 @@ def tile_attend_rel2_cap_topkq256n512t1024_kernel(tc, qT, k_words, k_scales, vT,
 
         def cap(h, c):
             nc.scalar.activation(
-                capped[h, c][:].rearrange("p (t s) -> p t s", t=2),
-                scores[h][:].rearrange("p (s t) -> p t s", t=PACK)[:, 2 * c : 2 * c + 2],
+                capped[h, c].rearrange("p (t s) -> p t s", t=2),
+                scores[h, c][:].rearrange("p (s t) -> p t s", t=2),
                 ACT.Tanh,
                 scale=1.0 / CAP,
             )
@@ -178,7 +182,7 @@ def tile_attend_rel2_cap_topkq256n512t1024_kernel(tc, qT, k_words, k_scales, vT,
         v_bf = [tile("v_bf0", [P, P, PACK], BF16, tag="v_pool1"), tile("v_bf1", [P, P, PACK], BF16)]
 
         def turn_values(e):
-            bank = ps.tile([P, PAIRS, P], F32, name=f"v_turned{e}", tag=f"scores{e}")
+            bank = ps.tile([P, PAIRS, P], F32, name=f"v_turned{e}", tag=f"v_turned{e}")
             words = v_got[e][:].bitcast(F32)
             for c in range(PAIRS):
                 nc.tensor.transpose(bank[:, c, :], words[:, c : N // 2 : PAIRS], ident[:])
@@ -191,9 +195,9 @@ def tile_attend_rel2_cap_topkq256n512t1024_kernel(tc, qT, k_words, k_scales, vT,
         for h, c in half_pair:
             nc.vector.scalar_tensor_tensor(
                 out=squares[h, c][:],
-                in0=capped[h, c][:],
+                in0=capped[h, c],
                 scalar=0.0,
-                in1=capped[h, c][:],
+                in1=capped[h, c],
                 op0=ALU.max,
                 op1=ALU.mult,
                 accum_out=sum_of(h, c),
@@ -230,7 +234,7 @@ def tile_attend_rel2_cap_topkq256n512t1024_kernel(tc, qT, k_words, k_scales, vT,
 
         for e in range(PLANES):
             for h in range(HALVES):
-                acc = ps.tile([P, P], F32, name=f"acc{h}{e}")
+                acc = ps.tile([P, P], F32, name=f"acc{h}{e}", tag=f"scores{h}{e}")
                 nc.tensor.matmul_mx(
                     out=acc[:],
                     lhsT=w_codes[h][:].bitcast(FP8X4),

from contextlib import ExitStack

import concourse.mybir as mybir
from concourse.masks import make_identity

F32 = mybir.dt.float32
BF16 = mybir.dt.bfloat16
I32 = mybir.dt.int32
U32 = mybir.dt.uint32
U16 = mybir.dt.uint16
U8 = mybir.dt.uint8
FP8X4 = mybir.dt.float8_e4m3fn_x4
FP4X4 = mybir.dt.float4_e2m1fn_x4
ACT = mybir.ActivationFunctionType
ALU = mybir.AluOpType

P = 128
QUADRANT = 32
PACK = 4
N, T, D, DV, NQ = 512, 1024, 1024, 256, 256
PASSES = D // (P * PACK)
HALVES = NQ // P
PLANES = DV // P
PAIRS = PACK // 2
CAP = 2.0
V_AHEAD = 384
V_SPLIT = 224

FLOPS = 2 * NQ * N * (D + DV)


def tile_attend_rel2_cap_topkq256n512t1024_kernel(tc, qT, k_words, k_scales, vT, vs, offs, out):
    nc = tc.nc
    with ExitStack() as ctx:
        sb = ctx.enter_context(tc.tile_pool(name="sb", bufs=1))
        ps = ctx.enter_context(tc.psum_pool(name="ps", bufs=1))

        def tile(name, shape, dtype, tag=None):
            return sb.tile(shape, dtype, name=name, tag=tag or name, align_bytes=64)

        offsets = sb.tile([P, N // 16], U16, name="offsets")

        def listed(lo, hi):
            return offsets[:, lo // 16 : hi // 16]

        q_rows = qT[0].rearrange("(o p t) q -> o p t q", p=P, t=PACK)
        q_raw = [tile(f"q_raw{o}", [P, PACK, NQ], F32) for o in range(PASSES)]

        vs_pool = tile("vs_pool", [P, T], F32)
        nc.vector.memset(vs_pool[:], 0.0)
        ks_pool = tile("ks_pool", [P, T // 4], I32)
        nc.sync.dma_start(ks_pool[:QUADRANT, :], k_scales.bitcast(I32).rearrange("o r t -> r o t"))
        nc.sync.dma_start(offsets[:], offs)
        kw_pool = tile("kw_pool", [P, T], I32)
        nc.sync.dma_start(kw_pool[:], k_words[0].rearrange("p t b -> p (t b)").bitcast(I32))
        nc.sync.dma_start(vs_pool[0:1, :], vs[0:1, :])
        nc.vector.memset(ks_pool[QUADRANT : 2 * QUADRANT, :], 0)
        nc.vector.memset(ks_pool[2 * QUADRANT :, :], 0)
        for o in range(PASSES):
            nc.sync.dma_start(q_raw[o][:], q_rows[o])

        table_in = sb.tile([P, 1], F32, name="table_in")
        table_out = sb.tile([P, 1], F32, name="table_out")
        nc.gpsimd.memset(table_in[:], 0.0)
        nc.scalar.activation(table_out[:], table_in[:], ACT.Tanh)

        ks_planes = tile("ks_planes", [P, PASSES * N // 4], I32)
        nc.vector.memset(ks_planes[:], 0)
        ident = tile("ident", [P, P], F32)
        nc.vector.memset(ident[:], 0.0)
        make_identity(nc, ident[:], nomemset=True)

        v_pool = [tile(f"v_pool{e}", [P, T], F32) for e in range(PLANES)]

        nc.sync.dma_start(v_pool[0][:, :V_AHEAD], vT[0:P, :V_AHEAD])

        vs_got = tile("vs_got", [P, N], F32)
        nc.scalar.activation(vs_got[:], vs_pool[:].indirect(offsets[:]), ACT.Copy)

        ks_got = tile("ks_got", [P, N], U8)
        nc.vector.tensor_copy(
            ks_got[:].rearrange("p (c s e) -> p s c e", c=PAIRS, e=2), ks_pool[:].bitcast(U8).indirect(offsets[:])
        )
        for g in range(P // QUADRANT):
            rows = ks_got[4 * PASSES * g : 4 * PASSES * (g + 1), :]
            nc.sync.dma_start(ks_planes[QUADRANT * g : QUADRANT * g + 4, :], rows.bitcast(I32))
        k_planes = [ks_planes[:].bitcast(U8)[:, o * N : (o + 1) * N] for o in range(PASSES)]
        nc.sync.dma_start(v_pool[0][:, V_AHEAD:], vT[0:P, V_AHEAD:])
        vs_cols = tile("vs_cols", [P, PACK], F32)
        nc.sync.dma_start(vs_cols[:], vs_got[0:1, :])
        nc.sync.dma_start(v_pool[1][:], vT[P : 2 * P, :])

        kw_got = tile("kw_got", [P, N], U32)
        slot_halves = [slice(0, N // 2), slice(N // 2, N)]
        for cols in slot_halves:
            nc.vector.tensor_copy(
                kw_got[:, cols], kw_pool[:].bitcast(U32).indirect(offsets[:, cols.start // 16 : cols.stop // 16])
            )
        k_codes = tile("k_codes", [P, PASSES, N], U16)
        dealt = k_codes[:].rearrange("p o (c s e) -> p o s c e", c=PAIRS, e=2)
        listed_words = kw_got[:].bitcast(U16).rearrange("p (s c e o) -> p o s c e", c=PAIRS, e=2, o=PASSES)
        for x in range(2):
            rows = slice(x * P // 2, (x + 1) * P // 2)
            nc.vector.tensor_copy(dealt[:, :, rows], listed_words[:, :, rows])

        pass_half = [(o, h) for o in range(PASSES) for h in range(HALVES)]
        q_bf = {(o, h): tile(f"q_bf{o}{h}", [P, P, PACK], BF16) for o, h in pass_half}
        q_codes = {(o, h): tile(f"q_codes{o}{h}", [P, P], U32) for o, h in pass_half}
        q_scales = {(o, h): tile(f"q_scales{o}{h}", [P, P], U8) for o, h in pass_half}
        q_halves = [slice(h * P, (h + 1) * P) for h in range(HALVES)]

        def cast(o, h, on_vector):
            dst = q_bf[o, h][:].rearrange("p (a b) t -> p a t b", b=4)
            src = q_raw[o][:, :, q_halves[h]].rearrange("p t (a b) -> p a t b", b=4)
            if on_vector:
                nc.vector.tensor_copy(dst, src)
            else:
                nc.scalar.activation(dst, src, ACT.Copy)

        def quantize(codes, scales, values):
            nc.vector.quantize_mx(out=codes.bitcast(FP8X4), scales=scales, in_=values.rearrange("p x t -> p (x t)"))

        def quantize_q(o, h):
            quantize(q_codes[o, h][:], q_scales[o, h][:], q_bf[o, h][:])

        cast(0, 0, False)
        cast(0, 1, False)
        cast(1, 0, True)
        quantize_q(0, 0)
        cast(1, 1, False)
        quantize_q(1, 0)
        quantize_q(0, 1)
        quantize_q(1, 1)

        half_pair = [(h, c) for h in range(HALVES) for c in range(PAIRS)]
        pair_cols = [slice(c * N // PAIRS, (c + 1) * N // PAIRS) for c in range(PAIRS)]
        scores = {(h, c): ps.tile([P, N // PAIRS], F32, name=f"scores{h}{c}", tag=f"scores{h}{c}") for h, c in half_pair}
        for h, c in half_pair:
            for o in range(PASSES):
                nc.tensor.matmul_mx(
                    out=scores[h, c][:],
                    lhsT=q_codes[o, h][:].bitcast(FP8X4),
                    lhsT_scale=q_scales[o, h][:],
                    rhs=k_codes[:, o, pair_cols[c]].bitcast(FP4X4),
                    rhs_scale=k_planes[o][:, pair_cols[c]],
                    start=(o == 0),
                    stop=(o == PASSES - 1),
                )

        v_got = [tile("v_got0", [P, N], BF16), tile("v_got1", [P, N], BF16)]
        nc.scalar.activation(v_got[0][:, :V_SPLIT], v_pool[0][:].indirect(listed(0, V_SPLIT)), ACT.Copy)
        nc.vector.tensor_copy(v_got[0][:, V_SPLIT:], v_pool[0][:].indirect(listed(V_SPLIT, N)))

        capped_all = tile("capped", [P, HALVES, N], F32, tag="vs_got")
        capped = {(h, c): capped_all[:, h, pair_cols[c]] for h, c in half_pair}
        squares = {(h, c): tile(f"squares{h}{c}", [P, N // PAIRS], F32) for h, c in half_pair}
        sums = tile("sums", [P, HALVES * PAIRS], F32)
        p_turned = [ps.tile([P, PACK, P], F32, name=f"p_turned{h}") for h in range(HALVES)]
        w_bf = [tile(f"w_bf{h}", [P, P, PACK], BF16) for h in range(HALVES)]
        w_scales = [tile(f"w_scales{h}", [P, P], U8) for h in range(HALVES)]

        def sum_of(h, c):
            return sums[:, PAIRS * h + c : PAIRS * h + c + 1]

        def cap(h, c):
            nc.scalar.activation(
                capped[h, c].rearrange("p (t s) -> p t s", t=2),
                scores[h, c][:].rearrange("p (s t) -> p t s", t=2),
                ACT.Tanh,
                scale=1.0 / CAP,
            )

        def gather_on_scalar(lo, hi):
            nc.scalar.activation(v_got[1][:, lo:hi], v_pool[1][:].indirect(listed(lo, hi)), ACT.Copy)

        cap(0, 0)
        cap(0, 1)
        cap(1, 0)
        cap(1, 1)
        gather_on_scalar(0, N)

        v_bf = [tile("v_bf0", [P, P, PACK], BF16, tag="v_pool1"), tile("v_bf1", [P, P, PACK], BF16)]

        def turn_values(e):
            bank = ps.tile([P, PAIRS, P], F32, name=f"v_turned{e}", tag=f"v_turned{e}")
            words = v_got[e][:].bitcast(F32)
            for c in range(PAIRS):
                nc.tensor.transpose(bank[:, c, :], words[:, c : N // 2 : PAIRS], ident[:])
            nc.scalar.copy(
                v_bf[e][:].rearrange("p f t -> p (f t)").bitcast(F32).rearrange("p (f c) -> p f c", c=PAIRS),
                bank[:].rearrange("p c f -> p f c"),
            )

        turn_values(0)
        for h, c in half_pair:
            nc.vector.scalar_tensor_tensor(
                out=squares[h, c][:],
                in0=capped[h, c],
                scalar=0.0,
                in1=capped[h, c],
                op0=ALU.max,
                op1=ALU.mult,
                accum_out=sum_of(h, c),
            )
            for t in range(2):
                nc.tensor.transpose(p_turned[h][:, 2 * c + t, :], squares[h, c][:, t * P : (t + 1) * P], ident[:])
        turn_values(1)

        totals = tile("totals", [P, HALVES], F32)
        inverse = tile("inverse", [P, HALVES], F32)
        pairs_of = sums[:].rearrange("p (h c) -> p h c", c=PAIRS)
        nc.vector.scalar_tensor_tensor(
            out=totals[:], in0=pairs_of[:, :, 0], scalar=1.0 / (CAP * CAP), in1=pairs_of[:, :, 1], op0=ALU.add, op1=ALU.add
        )

        v_codes = [tile("v_codes0", [P, P], U32), tile("v_codes1", [P, P], U32, tag="vs_cols")]
        v_scales = [tile(f"v_scales{e}", [P, P], U8) for e in range(PLANES)]
        w_codes = [tile(f"w_codes{h}", [P, P], U32) for h in range(HALVES)]

        def weigh(h):
            nc.vector.tensor_tensor(
                out=w_bf[h][:],
                in0=p_turned[h][:].rearrange("p t q -> p q t"),
                in1=vs_cols[:].unsqueeze(1).broadcast_to([P, P, PACK]),
                op=ALU.mult,
            )

        weigh(0)
        nc.vector.reciprocal(inverse[:], totals[:])
        weigh(1)
        for x in range(HALVES):
            quantize(w_codes[x][:], w_scales[x][:], w_bf[x][:])
            quantize(v_codes[x][:], v_scales[x][:], v_bf[x][:])

        for e in range(PLANES):
            for h in range(HALVES):
                acc = ps.tile([P, P], F32, name=f"acc{h}{e}", tag=f"scores{h}{e}")
                nc.tensor.matmul_mx(
                    out=acc[:],
                    lhsT=w_codes[h][:].bitcast(FP8X4),
                    lhsT_scale=w_scales[h][:],
                    rhs=v_codes[e][:].bitcast(FP8X4),
                    rhs_scale=v_scales[e][:],
                    start=True,
                    stop=True,
                )
                y = tile(f"y{h}{e}", [P, P], F32)
                last_plane = e == PLANES - 1
                if last_plane and h == 0:
                    nc.vector.tensor_scalar(y[:], acc[:], inverse[:, h : h + 1], None, ALU.mult)
                else:
                    nc.scalar.activation(y[:], acc[:], ACT.Copy, scale=inverse[:, h : h + 1])
                queue = nc.scalar if last_plane and h == 1 else nc.sync
                queue.dma_start(out[0, q_halves[h], e * P : (e + 1) * P], y[:])
